import numpy as np
import ml_dtypes


def mxq(x, axis, fmt="e4m3"):
    dtype, down = {"e4m3": (ml_dtypes.float8_e4m3fn, 7), "e5m2": (ml_dtypes.float8_e5m2, 14)}[fmt]
    v = np.moveaxis(np.asarray(x, np.float32).astype(ml_dtypes.bfloat16).astype(np.float64), axis, -1)
    blocks = v.reshape(v.shape[:-1] + (-1, 32))
    amax = np.abs(blocks).max(-1, keepdims=True)
    byte = np.maximum(np.where(amax > 0, np.frexp(amax)[1] - 1 + 127, 0) - down, 1)
    scale = np.exp2(byte - 127.0)
    codes = (blocks / scale).astype(np.float32).astype(dtype).astype(np.float64)
    return np.moveaxis((codes * scale).reshape(v.shape), -1, axis)


WIDE = False


def mx_kscale(k):
    if not WIDE:
        return np.ones(k)
    levels = np.array([10, -10, 5, -5, 0])
    if k % 512:
        return np.exp2(np.random.permutation(np.resize(levels, k // 32))).repeat(32)
    a = np.empty((k // 512, 16))
    for p in range(k // 512):
        a[p, :8] = np.random.permutation(np.resize(levels, 8))
        for g in range(8):
            far = levels[np.abs(levels - a[p, g]) >= 10]
            a[p, g + 8] = far[np.random.randint(len(far))]
    return np.exp2(a.ravel()).repeat(32)


def f64(x):
    return np.asarray(x).astype(np.float64)


def striped(idx):
    return np.tile(idx.reshape(-1, 16).T, (8, 1)).astype(np.uint16)


def unstriped(offs):
    return offs[:16].T.reshape(-1).astype(np.int64)


E2M1 = np.array([0.0, 0.5, 1.0, 1.5, 2.0, 3.0, 4.0, 6.0, -0.0, -0.5, -1.0, -1.5, -2.0, -3.0, -4.0, -6.0])


def pack_weight(w, fmt):
    k, n = w.shape
    w = f64(np.asarray(w, np.float32).astype(ml_dtypes.bfloat16)).reshape(k // 32, 32, n)
    amax = np.abs(w).max(1)
    if fmt == "e4m3":
        byte = np.frexp(amax)[1] - 1 + 127 - 7
    else:
        mant, ex = np.frexp(amax / 6.0)
        byte = np.where(mant > 0.5, ex, ex - 1) + 127
    byte = np.clip(np.where(amax > 0, byte, 1), 1, 254)
    scaled = (w * np.exp2(127.0 - byte)[:, None, :]).reshape(k, n).astype(np.float32)
    by_word = np.ascontiguousarray(scaled.reshape(k // 512, 128, 4, n).transpose(0, 1, 3, 2))
    if fmt == "e4m3":
        words = by_word.astype(ml_dtypes.float8_e4m3fn).view(np.uint8)
    else:
        c = by_word.astype(ml_dtypes.float4_e2m1fn).view(np.uint8) & 0xF
        words = (c[..., 0::2] | (c[..., 1::2] << 4)).reshape(k // 512, 128, 2 * n)
    return np.ascontiguousarray(words), np.ascontiguousarray(byte.astype(np.uint8).reshape(k // 512, 16, n))


def unpack_weight(words, scales, fmt):
    g, _, n = scales.shape
    words = np.ascontiguousarray(words).reshape(g, 128, n, -1)
    if fmt == "e4m3":
        vals = words.view(ml_dtypes.float8_e4m3fn).astype(np.float64)
    else:
        nib = np.empty((g, 128, n, 4), np.uint8)
        nib[..., 0::2] = words & 0xF
        nib[..., 1::2] = words >> 4
        vals = E2M1[nib]
    vals = vals * np.repeat(np.exp2(scales.astype(np.float64) - 127.0), 8, axis=1)[..., None]
    return vals.transpose(0, 1, 3, 2).reshape(g * 512, n)


def gelu(v):
    return 0.5 * v * (1.0 + np.tanh(np.sqrt(2.0 / np.pi) * (v + 0.044715 * v**3)))


def bf(x):
    return np.asarray(x, np.float32).astype(ml_dtypes.bfloat16)

def planes(Y):
    n, m = Y.shape
    b = f64(bf(Y)).reshape(n // 32, 32, m)
    amax = np.abs(b).max(1)
    byte = np.clip(np.where(amax > 0, np.frexp(amax)[1] - 1 + 127 - 7, 1), 1, 254)
    codes = (b * np.exp2(127.0 - byte)[:, None, :]).reshape(n, m).astype(np.float32).astype(ml_dtypes.float8_e4m3fn).view(np.uint8)
    words = codes.reshape(n // 512, 128, 4, m).transpose(0, 1, 3, 2)
    return np.ascontiguousarray(words), np.ascontiguousarray(byte.astype(np.uint8).reshape(n // 512, 16, m))


K, H, N, T, S = 1024, 1024, 512, 2048, 1024

def setup_inputs():
    n = np.random.standard_normal
    s = mx_kscale(K)[:, None]
    u = mx_kscale(H)[:, None]
    tab_words, tab_scales = pack_weight(n((K, T)) * s, "e4m3")
    offs = striped(np.random.permutation(T)[:S])
    w1 = (n((K, H)) / np.sqrt(K) / s).astype(np.float32)
    gT = np.exp(0.3 * n((H, T))).astype(np.float32)
    pre = (np.exp(0.3 * n(H)) * u[:, 0]).astype(np.float32)
    gain = np.exp(0.8 * n(N))[None, :]
    wnu_words, wnu_scales = pack_weight(1.5 * n((H, N)) / np.sqrt(H) * gain / u, "e2m1")
    return {"tab_words": tab_words, "tab_scales": tab_scales, "offs": offs, "w1": w1, "gT": gT,
            "pre": pre, "wnu_words": wnu_words, "wnu_scales": wnu_scales}

def reference(tab_words, tab_scales, offs, w1, gT, pre, wnu_words, wnu_scales):
    v = unpack_weight(tab_words, tab_scales, "e4m3")[:, unstriped(offs)]
    g = f64(gT)[:, unstriped(offs)]
    e = np.abs(mxq(f64(w1), 0, "e4m3").T @ v)
    h = f64(pre)[:, None] * np.exp(-(e / g))
    wnu = unpack_weight(wnu_words, wnu_scales, "e2m1")
    y = wnu.T @ mxq(h, 0, "e4m3")
    words, scales = planes(y)
    return y, words, scales

@@ -1,0 +1,299 @@
+from contextlib import ExitStack
+
+import concourse.mybir as mybir
+
+K, H, N, T, S = 1024, 1024, 512, 2048, 1024
+FLOPS = 2 * K * H * S + 2 * H * N * S
+
+F32 = mybir.dt.float32
+BF16 = mybir.dt.bfloat16
+I32 = mybir.dt.int32
+U32 = mybir.dt.uint32
+U16 = mybir.dt.uint16
+U8 = mybir.dt.uint8
+FP8X4 = mybir.dt.float8_e4m3fn_x4
+FP4X4 = mybir.dt.float4_e2m1fn_x4
+ACT = mybir.ActivationFunctionType
+ALU = mybir.AluOpType
+
+P = 128
+PACK = 4
+PASS = P * PACK
+BANK = 512
+CHUNK = 256
+SUB = 128
+QUADS = 4
+PINS = {(0, 0): 3, (1, 0): 4}
+WORD_STORES = {768: 0, 1024: 768}
+
+
+def tile_list_arrhenius_source_terms_kernel(
+    tc, tab_words, tab_scales, offs, w1, gT, pre, wnu_words, wnu_scales, out_0, out_1, out_2
+):
+    nc = tc.nc
+    chunks = S // CHUNK
+
+    with ExitStack() as ctx:
+        keep = ctx.enter_context(tc.tile_pool(name="keep", bufs=1))
+        ring = ctx.enter_context(tc.tile_pool(name="ring", bufs=1))
+        psum = ctx.enter_context(tc.psum_pool(name="psum", bufs=8))
+
+        offsets = keep.tile([P, S // 16], U16, name="offsets")
+        nc.sync.dma_start(offsets[:], offs)
+
+        tab_plane = keep.tile([P, T], U8, name="tab_plane", align_bytes=64)
+        wnu_plane_raw = keep.tile([P, 2, N], U8, name="wnu_plane_raw", align_bytes=64)
+        nc.vector.memset(wnu_plane_raw[:].bitcast(I32), 0)
+        nc.vector.memset(tab_plane[:].bitcast(I32), 0)
+
+        all_temps = keep.tile([P, 2 * PACK, S], F32, name="temps")
+        temps = [all_temps[:, b * PACK : (b + 1) * PACK, :] for b in range(2)]
+        energy = [keep.tile([P, PACK, S], F32, name="energy%d" % b) for b in range(2)]
+        g_rows = gT.rearrange("(b p t) c -> b t p c", p=P, t=PACK)
+
+        windows = {}
+
+        def load_g(b, t):
+            win = ring.tile([P, T], F32, name="g_window", tag="slot%d" % ((b * PACK + t) % 5), align_bytes=64)
+            nc.sync.dma_start(win[:], g_rows[b, t])
+            windows[b, t] = win
+
+        def gather_g(b, t):
+            nc.vector.tensor_copy(temps[b][:, t, :], windows[b, t][:].indirect(offsets[:]))
+
+        def log_g(b, t):
+            nc.scalar.activation(temps[b][:, t, :], temps[b][:, t, :], ACT.Ln)
+
+        w_raw, w_round, w_codes, w_scales = {}, {}, {}, {}
+
+        def load_w(a, b):
+            raw = ring.tile([P, PACK, PASS], F32, name="w_raw", bufs=3)
+            rows = w1[a * PASS : (a + 1) * PASS, b * PASS : (b + 1) * PASS]
+            nc.sync.dma_start(raw[:], rows.rearrange("(p j) c -> p j c", j=PACK))
+            w_raw[a, b] = raw
+
+        def round_w(a, b, copy):
+            grouped = ring.tile([P, PASS * PACK], BF16, name="w_round", bufs=2, align_bytes=64)
+            copy(
+                grouped[:].rearrange("p (t m j) -> p m j t", t=PACK, j=PACK),
+                w_raw[a, b][:].rearrange("p j (m t) -> p m j t", t=PACK),
+            )
+            w_round[a, b] = grouped
+
+        def quantize_w(a, b):
+            if (a, b) in PINS:
+                codes = ring.tile([P, PASS], I32, name="w_codes", tag="slot%d" % PINS[a, b], align_bytes=64)
+            else:
+                codes = keep.tile([P, PASS], I32, name="w_codes%d%d" % (a, b), align_bytes=64)
+            scales = keep.tile([P, PASS], U8, name="w_scales%d%d" % (a, b), align_bytes=64)
+            nc.vector.quantize_mx(codes[:].bitcast(FP8X4), scales[:], w_round[a, b][:])
+            w_codes[a, b], w_scales[a, b] = codes, scales
+
+        tab = [keep.tile([P, T], I32, name="tab%d" % a) for a in range(2)]
+        picked = [keep.tile([P, S], I32, name="picked%d" % a, align_bytes=64) for a in range(2)]
+        picked_plane = keep.tile([P, S], U8, name="picked_plane", align_bytes=64)
+
+        def load_tab(a):
+            nc.sync.dma_start(tab[a][:], tab_words[a].rearrange("p c i -> p (c i)").bitcast(I32))
+
+        def gather_tab(a):
+            nc.vector.tensor_copy(picked[a][:].bitcast(U32), tab[a][:].bitcast(U32).indirect(offsets[:]))
+
+        def first_product(b, cols):
+            width = cols.stop - cols.start
+            per_bank = BANK // width
+            for t0 in range(0, PACK, per_bank):
+                acc = psum.tile([P, per_bank, width], F32, name="acc")
+                for t in range(t0, t0 + per_bank):
+                    m_cols = slice(t * P, (t + 1) * P)
+                    for a in range(2):
+                        nc.tensor.matmul_mx(
+                            acc[:, t - t0, :],
+                            lhsT=w_codes[a, b][:, m_cols].bitcast(FP8X4),
+                            lhsT_scale=w_scales[a, b][:, m_cols],
+                            rhs=picked[a][:, cols].bitcast(FP8X4),
+                            rhs_scale=picked_plane[4 * a : P, cols],
+                            start=(a == 0),
+                            stop=(a == 1),
+                        )
+                nc.scalar.activation(energy[b][:, t0 : t0 + per_bank, cols], acc[:], ACT.Abs)
+
+        def invert(cols):
+            nc.scalar.activation(all_temps[:, :, cols], all_temps[:, :, cols], ACT.Exp, scale=-1.0)
+
+        def divide(b, cols):
+            nc.vector.tensor_tensor(energy[b][:, :, cols], energy[b][:, :, cols], temps[b][:, :, cols], ALU.mult)
+
+        def decay(b, cols):
+            nc.scalar.activation(temps[b][:, :, cols], energy[b][:, :, cols], ACT.Exp, scale=-1.0)
+
+        factors = keep.tile([P, 2, PACK], F32, name="factors")
+        h_codes = [keep.tile([P, S], I32, name="h_codes%d" % b, align_bytes=64) for b in range(2)]
+        h_scales = [keep.tile([P, S], U8, name="h_scales%d" % b, align_bytes=64) for b in range(2)]
+        h_round = {}
+
+        def round_h(b, cols):
+            width = cols.stop - cols.start
+            grouped = ring.tile([P, width * PACK], BF16, name="h_round", bufs=3, align_bytes=64)
+            nc.vector.tensor_tensor(
+                grouped[:].rearrange("p (c i t) -> p c t i", i=2, t=PACK),
+                temps[b][:, :, cols].rearrange("p t (c i) -> p c t i", i=2),
+                factors[:, b, :].unsqueeze(1).unsqueeze(3).to_broadcast([P, width // 2, PACK, 2]),
+                ALU.mult,
+            )
+            h_round[b, cols.start] = grouped
+
+        def quantize_h(b, cols):
+            nc.vector.quantize_mx(h_codes[b][:, cols].bitcast(FP8X4), h_scales[b][:, cols], h_round[b, cols.start][:])
+
+        wnu_raw = keep.tile([P, 2, 2 * N], U8, name="wnu_raw", align_bytes=64)
+        wnu_codes = keep.tile([P, 2, PACK, 2 * P], U8, name="wnu_codes", align_bytes=64)
+        wnu_plane = keep.tile([P, 2, PACK, P], U8, name="wnu_plane", align_bytes=64)
+
+        def deal_wnu():
+            nc.vector.tensor_copy(
+                wnu_codes[:].rearrange("p a t (m e) -> p a m t e", e=2),
+                wnu_raw[:].rearrange("p a (m t e) -> p a m t e", t=PACK, e=2),
+            )
+            nc.vector.tensor_copy(
+                wnu_plane[:].rearrange("p a t m -> p a m t"),
+                wnu_plane_raw[:].rearrange("p a (m t) -> p a m t", t=PACK),
+            )
+
+        banks = {}
+
+        def second_product(b, cols):
+            for c0 in range(cols.start, cols.stop, SUB):
+                if b == 0:
+                    banks[c0] = psum.tile([P, PACK, SUB], F32, name="acc")
+                sub = slice(c0, c0 + SUB)
+                for t in range(PACK):
+                    nc.tensor.matmul_mx(
+                        banks[c0][:, t, :],
+                        lhsT=wnu_codes[:, b, t, :].bitcast(FP4X4),
+                        lhsT_scale=wnu_plane[:, b, t, :],
+                        rhs=h_codes[b][:, sub].bitcast(FP8X4),
+                        rhs_scale=h_scales[b][:, sub],
+                        start=(b == 0 and t == 0),
+                        stop=(b == 1 and t == PACK - 1),
+                    )
+
+        y_rows = out_0.rearrange("(p t) c -> p t c", t=PACK)
+        y_words = out_1[0].rearrange("p c t -> p (c t)").bitcast(I32)
+        y_plane = keep.tile([P, S], U8, name="y_plane", align_bytes=64)
+        y_codes = keep.tile([P, S], I32, name="y_codes", align_bytes=64)
+        y_full, y_round = {}, {}
+
+        def copy_y(cols):
+            width = cols.stop - cols.start
+            y = ring.tile([P, PACK, width], F32, name="y", bufs=4)
+            for c0 in range(0, width, SUB):
+                nc.scalar.copy(y[:, :, c0 : c0 + SUB], banks[cols.start + c0][:])
+            nc.sync.dma_start(y_rows[:, :, cols], y[:])
+            y_full[cols.start] = y
+
+        def round_y(cols):
+            width = cols.stop - cols.start
+            grouped = ring.tile([P, width * PACK], BF16, name="y_round", bufs=2, align_bytes=64)
+            nc.vector.tensor_copy(
+                grouped[:].rearrange("p (c i t) -> p c t i", i=4, t=PACK),
+                y_full[cols.start][:].rearrange("p t (c i) -> p c t i", i=4),
+            )
+            y_round[cols.start] = grouped
+
+        def quantize_y(cols):
+            nc.vector.quantize_mx(y_codes[:, cols].bitcast(FP8X4), y_plane[:, cols], y_round[cols.start][:])
+            if cols.stop in WORD_STORES:
+                done = slice(WORD_STORES[cols.stop], cols.stop)
+                nc.sync.dma_start(y_words[:, done], y_codes[:, done])
+
+        def load_wnu_words(queue):
+            queue.dma_start(wnu_raw[:].bitcast(I32), wnu_words.rearrange("a p c -> p a c").bitcast(I32))
+
+        def load_wnu_scales(queue):
+            for q in range(QUADS):
+                queue.dma_start(
+                    wnu_plane_raw[32 * q : 32 * q + 4].bitcast(I32),
+                    wnu_scales[:, 4 * q : 4 * q + 4, :].rearrange("a r c -> r a c").bitcast(I32),
+                )
+
+        def load_tab_scales(queue):
+            for q in range(QUADS):
+                queue.dma_start(
+                    tab_plane[32 * q : 32 * q + 8, :].bitcast(I32),
+                    tab_scales[:, 4 * q : 4 * q + 4, :].bitcast(I32),
+                )
+
+        def load_factors(queue):
+            queue.dma_start(factors[:], pre.rearrange("(b p t) -> p b t", p=P, t=PACK))
+
+        def gather_tab_scales():
+            nc.vector.tensor_copy(picked_plane[:], tab_plane[:].indirect(offsets[:]))
+
+        def store_y_scales():
+            for q in range(QUADS):
+                nc.sync.dma_start(
+                    out_2[0, 4 * q : 4 * q + 4, :].bitcast(I32), y_plane[32 * q : 32 * q + 4, :].bitcast(I32)
+                )
+
+        quarters = [slice(c, c + 256) for c in range(0, S, 256)]
+        load_g(0, 0)
+        load_g(0, 1)
+        load_tab_scales(nc.sync)
+        load_w(0, 0)
+        load_g(0, 2)
+        load_g(0, 3)
+        load_w(1, 0)
+        load_g(1, 0)
+        load_g(1, 1)
+        load_g(1, 2)
+        load_g(1, 3)
+        load_tab(0)
+        load_w(0, 1)
+        load_w(1, 1)
+        load_tab(1)
+        load_wnu_words(nc.sync)
+        load_wnu_scales(nc.sync)
+        load_factors(nc.sync)
+        gather_g(0, 0)
+        log_g(0, 0)
+        gather_g(0, 1)
+        log_g(0, 1)
+        round_w(0, 0, nc.scalar.copy)
+        gather_tab_scales()
+        gather_g(0, 2)
+        log_g(0, 2)
+        gather_g(0, 3)
+        log_g(0, 3)
+        quantize_w(0, 0)
+        round_w(1, 0, nc.scalar.copy)
+        gather_g(1, 0)
+        log_g(1, 0)
+        quantize_w(1, 0)
+        gather_g(1, 1)
+        log_g(1, 1)
+        gather_g(1, 2)
+        log_g(1, 2)
+        gather_g(1, 3)
+        log_g(1, 3)
+        gather_tab(0)
+        round_w(0, 1, nc.vector.tensor_copy)
+        quantize_w(0, 1)
+        round_w(1, 1, nc.vector.tensor_copy)
+        quantize_w(1, 1)
+        gather_tab(1)
+        deal_wnu()
+        pieces = [slice(0, 256), slice(256, 512), slice(512, 768), slice(768, 896), slice(896, 1024)]
+        units = [(b, cols) for cols in pieces for b in range(2)]
+        for step in range(len(units) + 8):
+            if step in [0,1,3,5,7]:
+                invert(pieces[[0,1,3,5,7].index(step)])
+            for stage, lag in ((decay, 2), (first_product, 0), (round_h, 3), (divide, 1), (quantize_h, 4), (second_product, 4), (copy_y, 5), (round_y, 6), (quantize_y, 7)):
+                if 0 <= step - lag < len(units):
+                    b, cols = units[step - lag]
+                    if stage in (copy_y, round_y, quantize_y):
+                        if b == 1:
+                            stage(cols)
+                    else:
+                        stage(b, cols)
+        store_y_scales()

@@ -23,7 +23,10 @@ BANK = 512
 CHUNK = 256
 SUB = 128
 QUADS = 4
-PINS = {(0, 0): 3, (1, 0): 4}
+ON_VECTOR = ()
+WINDOWS = 6
+ON_SCALAR = ()
+PINS = {(0, 0): 2, (1, 0): 3}
 WORD_STORES = {768: 0, 1024: 768}
 
 
@@ -46,15 +49,14 @@ def tile_list_arrhenius_source_terms_kernel(
         nc.vector.memset(wnu_plane_raw[:].bitcast(I32), 0)
         nc.vector.memset(tab_plane[:].bitcast(I32), 0)
 
-        all_temps = keep.tile([P, 2 * PACK, S], F32, name="temps")
-        temps = [all_temps[:, b * PACK : (b + 1) * PACK, :] for b in range(2)]
+        temps = [keep.tile([P, PACK, S], F32, name="temps%d" % b) for b in range(2)]
         energy = [keep.tile([P, PACK, S], F32, name="energy%d" % b) for b in range(2)]
         g_rows = gT.rearrange("(b p t) c -> b t p c", p=P, t=PACK)
 
         windows = {}
 
         def load_g(b, t):
-            win = ring.tile([P, T], F32, name="g_window", tag="slot%d" % ((b * PACK + t) % 5), align_bytes=64)
+            win = ring.tile([P, T], F32, name="g_window", tag="slot%d" % ((b * PACK + t) % WINDOWS), align_bytes=64)
             nc.sync.dma_start(win[:], g_rows[b, t])
             windows[b, t] = win
 
@@ -62,12 +64,12 @@ def tile_list_arrhenius_source_terms_kernel(
             nc.vector.tensor_copy(temps[b][:, t, :], windows[b, t][:].indirect(offsets[:]))
 
         def log_g(b, t):
-            nc.scalar.activation(temps[b][:, t, :], temps[b][:, t, :], ACT.Ln)
+            nc.scalar.activation(energy[1][:, t, :], temps[b][:, t, :], ACT.Ln)
 
         w_raw, w_round, w_codes, w_scales = {}, {}, {}, {}
 
         def load_w(a, b):
-            raw = ring.tile([P, PACK, PASS], F32, name="w_raw", bufs=3)
+            raw = ring.tile([P, PACK, PASS], F32, name="w_raw", tag="raw%d" % a)
             rows = w1[a * PASS : (a + 1) * PASS, b * PASS : (b + 1) * PASS]
             nc.sync.dma_start(raw[:], rows.rearrange("(p j) c -> p j c", j=PACK))
             w_raw[a, b] = raw
@@ -118,14 +120,21 @@ def tile_list_arrhenius_source_terms_kernel(
                         )
                 nc.scalar.activation(energy[b][:, t0 : t0 + per_bank, cols], acc[:], ACT.Abs)
 
-        def invert(cols):
-            nc.scalar.activation(all_temps[:, :, cols], all_temps[:, :, cols], ACT.Exp, scale=-1.0)
+        def invert(b, cols):
+            nc.scalar.activation(temps[0][:, :, cols], energy[1][:, :, cols], ACT.Exp, scale=-1.0)
+
+        ratios = [None, energy[1]]
+
+        def ratio(b, cols):
+            if ratios[b] is None:
+                ratios[b] = ring.tile([P, PACK, S], F32, name="ratio", tag="slot1", align_bytes=64)
+            return ratios[b][:, :, cols]
 
         def divide(b, cols):
-            nc.vector.tensor_tensor(energy[b][:, :, cols], energy[b][:, :, cols], temps[b][:, :, cols], ALU.mult)
+            nc.vector.tensor_tensor(ratio(b, cols), energy[b][:, :, cols], temps[0][:, :, cols], ALU.mult)
 
         def decay(b, cols):
-            nc.scalar.activation(temps[b][:, :, cols], energy[b][:, :, cols], ACT.Exp, scale=-1.0)
+            nc.scalar.activation(temps[1 - b][:, :, cols], ratio(b, cols), ACT.Exp, scale=-1.0)
 
         factors = keep.tile([P, 2, PACK], F32, name="factors")
         h_codes = [keep.tile([P, S], I32, name="h_codes%d" % b, align_bytes=64) for b in range(2)]
@@ -137,7 +146,7 @@ def tile_list_arrhenius_source_terms_kernel(
             grouped = ring.tile([P, width * PACK], BF16, name="h_round", bufs=3, align_bytes=64)
             nc.vector.tensor_tensor(
                 grouped[:].rearrange("p (c i t) -> p c t i", i=2, t=PACK),
-                temps[b][:, :, cols].rearrange("p t (c i) -> p c t i", i=2),
+                temps[1 - b][:, :, cols].rearrange("p t (c i) -> p c t i", i=2),
                 factors[:, b, :].unsqueeze(1).unsqueeze(3).to_broadcast([P, width // 2, PACK, 2]),
                 ALU.mult,
             )
@@ -152,8 +161,8 @@ def tile_list_arrhenius_source_terms_kernel(
 
         def deal_wnu():
             nc.vector.tensor_copy(
-                wnu_codes[:].rearrange("p a t (m e) -> p a m t e", e=2),
-                wnu_raw[:].rearrange("p a (m t e) -> p a m t e", t=PACK, e=2),
+                wnu_codes[:].bitcast(U16).rearrange("p a t m -> p a m t"),
+                wnu_raw[:].bitcast(U16).rearrange("p a (m t) -> p a m t", t=PACK),
             )
             nc.vector.tensor_copy(
                 wnu_plane[:].rearrange("p a t m -> p a m t"),
@@ -162,43 +171,54 @@ def tile_list_arrhenius_source_terms_kernel(
 
         banks = {}
 
-        def second_product(b, cols):
+        def second_product(cols):
             for c0 in range(cols.start, cols.stop, SUB):
-                if b == 0:
-                    banks[c0] = psum.tile([P, PACK, SUB], F32, name="acc")
+                banks[c0] = psum.tile([P, PACK, SUB], F32, name="acc")
                 sub = slice(c0, c0 + SUB)
-                for t in range(PACK):
-                    nc.tensor.matmul_mx(
-                        banks[c0][:, t, :],
-                        lhsT=wnu_codes[:, b, t, :].bitcast(FP4X4),
-                        lhsT_scale=wnu_plane[:, b, t, :],
-                        rhs=h_codes[b][:, sub].bitcast(FP8X4),
-                        rhs_scale=h_scales[b][:, sub],
-                        start=(b == 0 and t == 0),
-                        stop=(b == 1 and t == PACK - 1),
-                    )
+                for b in range(2):
+                    for t in range(PACK):
+                        nc.tensor.matmul_mx(
+                            banks[c0][:, t, :],
+                            lhsT=wnu_codes[:, b, t, :].bitcast(FP4X4),
+                            lhsT_scale=wnu_plane[:, b, t, :],
+                            rhs=h_codes[b][:, sub].bitcast(FP8X4),
+                            rhs_scale=h_scales[b][:, sub],
+                            start=(b == 0 and t == 0),
+                            stop=(b == 1 and t == PACK - 1),
+                        )
 
         y_rows = out_0.rearrange("(p t) c -> p t c", t=PACK)
         y_words = out_1[0].rearrange("p c t -> p (c t)").bitcast(I32)
         y_plane = keep.tile([P, S], U8, name="y_plane", align_bytes=64)
         y_codes = keep.tile([P, S], I32, name="y_codes", align_bytes=64)
-        y_full, y_round = {}, {}
+        y_halves, y_full, y_round = {}, {}, {}
 
         def copy_y(cols):
             width = cols.stop - cols.start
-            y = ring.tile([P, PACK, width], F32, name="y", bufs=4)
+            half = cols.start // BANK
+            if half not in y_halves:
+                y_halves[half] = ring.tile([P, PACK, BANK], F32, name="y", tag="y%d" % half)
+            y = y_halves[half][:, :, cols.start - half * BANK : cols.stop - half * BANK]
             for c0 in range(0, width, SUB):
-                nc.scalar.copy(y[:, :, c0 : c0 + SUB], banks[cols.start + c0][:])
-            nc.sync.dma_start(y_rows[:, :, cols], y[:])
+                copy = nc.vector.tensor_copy if cols.start + c0 in ON_VECTOR else nc.scalar.copy
+                copy(y[:, :, c0 : c0 + SUB], banks[cols.start + c0][:])
+            nc.sync.dma_start(y_rows[:, :, cols], y)
             y_full[cols.start] = y
 
         def round_y(cols):
             width = cols.stop - cols.start
             grouped = ring.tile([P, width * PACK], BF16, name="y_round", bufs=2, align_bytes=64)
-            nc.vector.tensor_copy(
-                grouped[:].rearrange("p (c i t) -> p c t i", i=4, t=PACK),
-                y_full[cols.start][:].rearrange("p t (c i) -> p c t i", i=4),
-            )
+            if cols.start in ON_SCALAR:
+                for c0 in range(0, width, SUB):
+                    nc.scalar.copy(
+                        grouped[:, c0 * PACK : (c0 + SUB) * PACK].rearrange("p (c t) -> p c t", t=PACK),
+                        banks[cols.start + c0][:].rearrange("p t c -> p c t"),
+                    )
+            else:
+                nc.vector.tensor_copy(
+                    grouped[:].rearrange("p (c i t) -> p c t i", i=4, t=PACK),
+                    y_full[cols.start].rearrange("p t (c i) -> p c t i", i=4),
+                )
             y_round[cols.start] = grouped
 
         def quantize_y(cols):
@@ -242,16 +262,16 @@ def tile_list_arrhenius_source_terms_kernel(
         load_tab_scales(nc.sync)
         load_w(0, 0)
         load_g(0, 2)
-        load_g(0, 3)
         load_w(1, 0)
+        load_g(0, 3)
+        load_tab(0)
+        load_tab(1)
         load_g(1, 0)
         load_g(1, 1)
         load_g(1, 2)
         load_g(1, 3)
-        load_tab(0)
         load_w(0, 1)
         load_w(1, 1)
-        load_tab(1)
         load_wnu_words(nc.sync)
         load_wnu_scales(nc.sync)
         load_factors(nc.sync)
@@ -263,37 +283,39 @@ def tile_list_arrhenius_source_terms_kernel(
         gather_tab_scales()
         gather_g(0, 2)
         log_g(0, 2)
-        gather_g(0, 3)
-        log_g(0, 3)
         quantize_w(0, 0)
         round_w(1, 0, nc.scalar.copy)
+        gather_g(0, 3)
+        log_g(0, 3)
+        quantize_w(1, 0)
+        gather_tab(0)
+        gather_tab(1)
+        for cols in quarters:
+            invert(0, cols)
+        for cols in (slice(0, 512), slice(512, 1024)): first_product(0, cols)
         gather_g(1, 0)
         log_g(1, 0)
-        quantize_w(1, 0)
         gather_g(1, 1)
         log_g(1, 1)
         gather_g(1, 2)
         log_g(1, 2)
         gather_g(1, 3)
         log_g(1, 3)
-        gather_tab(0)
         round_w(0, 1, nc.vector.tensor_copy)
         quantize_w(0, 1)
         round_w(1, 1, nc.vector.tensor_copy)
         quantize_w(1, 1)
-        gather_tab(1)
         deal_wnu()
-        pieces = [slice(0, 256), slice(256, 512), slice(512, 768), slice(768, 896), slice(896, 1024)]
-        units = [(b, cols) for cols in pieces for b in range(2)]
-        for step in range(len(units) + 8):
-            if step in [0,1,3,5,7]:
-                invert(pieces[[0,1,3,5,7].index(step)])
-            for stage, lag in ((decay, 2), (first_product, 0), (round_h, 3), (divide, 1), (quantize_h, 4), (second_product, 4), (copy_y, 5), (round_y, 6), (quantize_y, 7)):
+        first = [slice(0, 512), slice(512, 1024)]
+        second = [slice(0, 256), slice(256, 512), slice(512, 768), slice(768, 896), slice(896, 1024)]
+        units = [(b, (first, second)[b][i]) for b, i in [(0,0),(0,1),(1,0),(1,1),(1,2),(1,3),(1,4)]]
+        for step in range(len(units) + 12):
+            for stage, lag in ((decay, 2), (invert, 0), (first_product, 0), (round_h, 3), (divide, 1), (quantize_h, 4), (second_product, 4), (copy_y, 5), (round_y, 6), (quantize_y, 7)):
                 if 0 <= step - lag < len(units):
                     b, cols = units[step - lag]
-                    if stage in (copy_y, round_y, quantize_y):
+                    if stage in (second_product, copy_y, round_y, quantize_y):
                         if b == 1:
                             stage(cols)
-                    else:
+                    elif b == 1 or stage not in (invert, first_product):
                         stage(b, cols)
         store_y_scales()

@@ -64,7 +64,7 @@ def tile_list_arrhenius_source_terms_kernel(
             nc.vector.tensor_copy(temps[b][:, t, :], windows[b, t][:].indirect(offsets[:]))
 
         def log_g(b, t):
-            nc.scalar.activation(energy[1][:, t, :], temps[b][:, t, :], ACT.Ln)
+            nc.scalar.activation(energy[1][:, t, :], temps[b][:, t, :], ACT.Abs_reciprocal_sqrt)
 
         w_raw, w_round, w_codes, w_scales = {}, {}, {}, {}
 
@@ -121,7 +121,7 @@ def tile_list_arrhenius_source_terms_kernel(
                 nc.scalar.activation(energy[b][:, t0 : t0 + per_bank, cols], acc[:], ACT.Abs)
 
         def invert(b, cols):
-            nc.scalar.activation(temps[0][:, :, cols], energy[1][:, :, cols], ACT.Exp, scale=-1.0)
+            nc.scalar.activation(temps[0][:, :, cols], energy[1][:, :, cols], ACT.Square)
 
         ratios = [None, energy[1]]
 

@@ -25,8 +25,9 @@ SUB = 128
 QUADS = 4
 ON_VECTOR = ()
 WINDOWS = 6
+WINDOW_BYTES = 4 * T
 ON_SCALAR = ()
-PINS = {(0, 0): 2, (1, 0): 3}
+SQUARES_ON_GPSIMD = ((0, 1), (0, 3))
 WORD_STORES = {768: 0, 1024: 768}
 
 
@@ -39,6 +40,7 @@ def tile_list_arrhenius_source_terms_kernel(
     with ExitStack() as ctx:
         keep = ctx.enter_context(tc.tile_pool(name="keep", bufs=1))
         ring = ctx.enter_context(tc.tile_pool(name="ring", bufs=1))
+        hand = ctx.enter_context(tc.tile_pool(name="hand", bufs=1))
         psum = ctx.enter_context(tc.psum_pool(name="psum", bufs=8))
 
         offsets = keep.tile([P, S // 16], U16, name="offsets")
@@ -46,30 +48,43 @@ def tile_list_arrhenius_source_terms_kernel(
 
         tab_plane = keep.tile([P, T], U8, name="tab_plane", align_bytes=64)
         wnu_plane_raw = keep.tile([P, 2, N], U8, name="wnu_plane_raw", align_bytes=64)
-        nc.vector.memset(wnu_plane_raw[:].bitcast(I32), 0)
         nc.vector.memset(tab_plane[:].bitcast(I32), 0)
+        nc.vector.memset(wnu_plane_raw[:].bitcast(I32), 0)
 
         temps = [keep.tile([P, PACK, S], F32, name="temps%d" % b) for b in range(2)]
-        energy = [keep.tile([P, PACK, S], F32, name="energy%d" % b) for b in range(2)]
+        energy = [keep.tile([P, PACK, S], F32, name="energy0")]
+        pieces = {}
         g_rows = gT.rearrange("(b p t) c -> b t p c", p=P, t=PACK)
 
         windows = {}
 
+        def window_at(b, t):
+            return ((b * PACK + t) % WINDOWS) * WINDOW_BYTES
+
+        def raw_at(a):
+            return (WINDOWS + a) * WINDOW_BYTES
+
         def load_g(b, t):
-            win = ring.tile([P, T], F32, name="g_window", tag="slot%d" % ((b * PACK + t) % WINDOWS), align_bytes=64)
+            win = hand.tile([P, T], F32, name="g_window%d%d" % (b, t), offset=window_at(b, t), align_bytes=64)
             nc.sync.dma_start(win[:], g_rows[b, t])
             windows[b, t] = win
 
         def gather_g(b, t):
             nc.vector.tensor_copy(temps[b][:, t, :], windows[b, t][:].indirect(offsets[:]))
 
-        def log_g(b, t):
-            nc.scalar.activation(energy[1][:, t, :], temps[b][:, t, :], ACT.Abs_reciprocal_sqrt)
+        def root_g(b, t):
+            nc.scalar.activation(temps[b][:, t, :], temps[b][:, t, :], ACT.Abs_reciprocal_sqrt)
+
+        def square_g(b, t):
+            if (b, t) in SQUARES_ON_GPSIMD:
+                nc.gpsimd.tensor_tensor(temps[b][:, t, :], temps[b][:, t, :], temps[b][:, t, :], ALU.mult)
+            else:
+                nc.scalar.activation(temps[b][:, t, :], temps[b][:, t, :], ACT.Square)
 
         w_raw, w_round, w_codes, w_scales = {}, {}, {}, {}
 
         def load_w(a, b):
-            raw = ring.tile([P, PACK, PASS], F32, name="w_raw", tag="raw%d" % a)
+            raw = hand.tile([P, PACK, PASS], F32, name="w_raw%d%d" % (a, b), offset=raw_at(a), align_bytes=64)
             rows = w1[a * PASS : (a + 1) * PASS, b * PASS : (b + 1) * PASS]
             nc.sync.dma_start(raw[:], rows.rearrange("(p j) c -> p j c", j=PACK))
             w_raw[a, b] = raw
@@ -83,10 +98,7 @@ def tile_list_arrhenius_source_terms_kernel(
             w_round[a, b] = grouped
 
         def quantize_w(a, b):
-            if (a, b) in PINS:
-                codes = ring.tile([P, PASS], I32, name="w_codes", tag="slot%d" % PINS[a, b], align_bytes=64)
-            else:
-                codes = keep.tile([P, PASS], I32, name="w_codes%d%d" % (a, b), align_bytes=64)
+            codes = keep.tile([P, PASS], I32, name="w_codes%d%d" % (a, b), align_bytes=64)
             scales = keep.tile([P, PASS], U8, name="w_scales%d%d" % (a, b), align_bytes=64)
             nc.vector.quantize_mx(codes[:].bitcast(FP8X4), scales[:], w_round[a, b][:])
             w_codes[a, b], w_scales[a, b] = codes, scales
@@ -101,40 +113,66 @@ def tile_list_arrhenius_source_terms_kernel(
         def gather_tab(a):
             nc.vector.tensor_copy(picked[a][:].bitcast(U32), tab[a][:].bitcast(U32).indirect(offsets[:]))
 
-        def first_product(b, cols):
+        signed = {}
+
+        def signed_ratio(t, cols):
+            if cols.start not in signed:
+                signed[cols.start] = keep.tile([P, PACK, BANK], F32, name="signed%d" % cols.start)
+            acc = psum.tile([P, BANK], F32, name="acc")
+            m_cols = slice(t * P, (t + 1) * P)
+            for a in range(2):
+                nc.tensor.matmul_mx(
+                    acc[:],
+                    lhsT=w_codes[a, 1][:, m_cols].bitcast(FP8X4),
+                    lhsT_scale=w_scales[a, 1][:, m_cols],
+                    rhs=picked[a][:, cols].bitcast(FP8X4),
+                    rhs_scale=picked_plane[4 * a : P, cols],
+                    start=(a == 0),
+                    stop=(a == 1),
+                )
+            nc.vector.tensor_tensor(signed[cols.start][:, t, :], acc[:], temps[1][:, t, cols], ALU.mult)
+
+        def unsign(b, cols):
             width = cols.stop - cols.start
-            per_bank = BANK // width
-            for t0 in range(0, PACK, per_bank):
-                acc = psum.tile([P, per_bank, width], F32, name="acc")
-                for t in range(t0, t0 + per_bank):
-                    m_cols = slice(t * P, (t + 1) * P)
-                    for a in range(2):
-                        nc.tensor.matmul_mx(
-                            acc[:, t - t0, :],
-                            lhsT=w_codes[a, b][:, m_cols].bitcast(FP8X4),
-                            lhsT_scale=w_scales[a, b][:, m_cols],
-                            rhs=picked[a][:, cols].bitcast(FP8X4),
-                            rhs_scale=picked_plane[4 * a : P, cols],
-                            start=(a == 0),
-                            stop=(a == 1),
-                        )
-                nc.scalar.activation(energy[b][:, t0 : t0 + per_bank, cols], acc[:], ACT.Abs)
+            half = cols.start // BANK * BANK
+            pieces[b, cols.start] = keep.tile([P, PACK, width], F32, name="piece%d" % cols.start)
+            nc.scalar.activation(pieces[b, cols.start][:], signed[half][:, :, cols.start - half : cols.stop - half], ACT.Abs)
 
-        def invert(b, cols):
-            nc.scalar.activation(temps[0][:, :, cols], energy[1][:, :, cols], ACT.Square)
+        sums = {}
 
-        ratios = [None, energy[1]]
+        def first_pass(a, t):
+            m_cols = slice(t * P, (t + 1) * P)
+            for c0 in range(0, S, BANK):
+                cols = slice(c0, c0 + BANK)
+                if a == 0:
+                    sums[t, c0] = psum.tile([P, BANK], F32, name="acc")
+                nc.tensor.matmul_mx(
+                    sums[t, c0][:],
+                    lhsT=w_codes[a, 0][:, m_cols].bitcast(FP8X4),
+                    lhsT_scale=w_scales[a, 0][:, m_cols],
+                    rhs=picked[a][:, cols].bitcast(FP8X4),
+                    rhs_scale=picked_plane[4 * a : P, cols],
+                    start=(a == 0),
+                    stop=(a == 1),
+                )
 
-        def ratio(b, cols):
-            if ratios[b] is None:
-                ratios[b] = ring.tile([P, PACK, S], F32, name="ratio", tag="slot1", align_bytes=64)
-            return ratios[b][:, :, cols]
+        def magnitude(t):
+            for c0 in range(0, S, BANK):
+                nc.scalar.activation(energy[0][:, t, c0 : c0 + BANK], sums[t, c0][:], ACT.Abs)
 
-        def divide(b, cols):
-            nc.vector.tensor_tensor(ratio(b, cols), energy[b][:, :, cols], temps[0][:, :, cols], ALU.mult)
+        last = window_at(1, PACK - 1)
+
+        def divide_slice(t):
+            nc.gpsimd.tensor_tensor(energy[0][:, t, :], energy[0][:, t, :], temps[0][:, t, :], ALU.mult)
 
         def decay(b, cols):
-            nc.scalar.activation(temps[1 - b][:, :, cols], ratio(b, cols), ACT.Exp, scale=-1.0)
+            if b == 0:
+                at = last - WINDOW_BYTES // 2 + 16 * cols.start
+                pieces[b, cols.start] = hand.tile([P, PACK, BANK], F32, name="decayed%d" % cols.start, offset=at, align_bytes=64)
+                ratio = energy[0][:, :, cols]
+            else:
+                ratio = pieces[b, cols.start][:]
+            nc.scalar.activation(pieces[b, cols.start][:], ratio, ACT.Exp, scale=-1.0)
 
         factors = keep.tile([P, 2, PACK], F32, name="factors")
         h_codes = [keep.tile([P, S], I32, name="h_codes%d" % b, align_bytes=64) for b in range(2)]
@@ -143,10 +181,15 @@ def tile_list_arrhenius_source_terms_kernel(
 
         def round_h(b, cols):
             width = cols.stop - cols.start
-            grouped = ring.tile([P, width * PACK], BF16, name="h_round", bufs=3, align_bytes=64)
+            if b == 0:
+                grouped = hand.tile(
+                    [P, width * PACK], BF16, name="h_round0_%d" % cols.start, offset=raw_at(1) + 8 * cols.start, align_bytes=64
+                )
+            else:
+                grouped = ring.tile([P, width * PACK], BF16, name="h_round", bufs=3, align_bytes=64)
             nc.vector.tensor_tensor(
                 grouped[:].rearrange("p (c i t) -> p c t i", i=2, t=PACK),
-                temps[1 - b][:, :, cols].rearrange("p t (c i) -> p c t i", i=2),
+                pieces[b, cols.start][:].rearrange("p t (c i) -> p c t i", i=2),
                 factors[:, b, :].unsqueeze(1).unsqueeze(3).to_broadcast([P, width // 2, PACK, 2]),
                 ALU.mult,
             )
@@ -191,14 +234,11 @@ def tile_list_arrhenius_source_terms_kernel(
         y_words = out_1[0].rearrange("p c t -> p (c t)").bitcast(I32)
         y_plane = keep.tile([P, S], U8, name="y_plane", align_bytes=64)
         y_codes = keep.tile([P, S], I32, name="y_codes", align_bytes=64)
-        y_halves, y_full, y_round = {}, {}, {}
+        y_full, y_round = {}, {}
 
         def copy_y(cols):
             width = cols.stop - cols.start
-            half = cols.start // BANK
-            if half not in y_halves:
-                y_halves[half] = ring.tile([P, PACK, BANK], F32, name="y", tag="y%d" % half)
-            y = y_halves[half][:, :, cols.start - half * BANK : cols.stop - half * BANK]
+            y = keep.tile([P, PACK, width], F32, name="y%d" % cols.start)[:]
             for c0 in range(0, width, SUB):
                 copy = nc.vector.tensor_copy if cols.start + c0 in ON_VECTOR else nc.scalar.copy
                 copy(y[:, :, c0 : c0 + SUB], banks[cols.start + c0][:])
@@ -256,66 +296,78 @@ def tile_list_arrhenius_source_terms_kernel(
                     out_2[0, 4 * q : 4 * q + 4, :].bitcast(I32), y_plane[32 * q : 32 * q + 4, :].bitcast(I32)
                 )
 
-        quarters = [slice(c, c + 256) for c in range(0, S, 256)]
-        load_g(0, 0)
-        load_g(0, 1)
-        load_tab_scales(nc.sync)
         load_w(0, 0)
-        load_g(0, 2)
-        load_w(1, 0)
-        load_g(0, 3)
+        load_tab_scales(nc.sync)
         load_tab(0)
+        load_wnu_words(nc.sync)
+        load_wnu_scales(nc.sync)
+        load_factors(nc.sync)
+        load_w(1, 0)
+        load_g(0, 0)
         load_tab(1)
+        load_g(0, 1)
+        load_g(0, 2)
+        load_g(0, 3)
         load_g(1, 0)
         load_g(1, 1)
         load_g(1, 2)
         load_g(1, 3)
         load_w(0, 1)
         load_w(1, 1)
-        load_wnu_words(nc.sync)
-        load_wnu_scales(nc.sync)
-        load_factors(nc.sync)
-        gather_g(0, 0)
-        log_g(0, 0)
-        gather_g(0, 1)
-        log_g(0, 1)
-        round_w(0, 0, nc.scalar.copy)
+
+        def invert_g(b, t):
+            gather_g(b, t)
+            root_g(b, t)
+            square_g(b, t)
+
         gather_tab_scales()
-        gather_g(0, 2)
-        log_g(0, 2)
-        quantize_w(0, 0)
-        round_w(1, 0, nc.scalar.copy)
-        gather_g(0, 3)
-        log_g(0, 3)
-        quantize_w(1, 0)
+        round_w(0, 0, nc.scalar.copy)
         gather_tab(0)
-        gather_tab(1)
-        for cols in quarters:
-            invert(0, cols)
-        for cols in (slice(0, 512), slice(512, 1024)): first_product(0, cols)
-        gather_g(1, 0)
-        log_g(1, 0)
-        gather_g(1, 1)
-        log_g(1, 1)
-        gather_g(1, 2)
-        log_g(1, 2)
-        gather_g(1, 3)
-        log_g(1, 3)
-        round_w(0, 1, nc.vector.tensor_copy)
-        quantize_w(0, 1)
-        round_w(1, 1, nc.vector.tensor_copy)
-        quantize_w(1, 1)
+        quantize_w(0, 0)
         deal_wnu()
+        for t in range(PACK):
+            first_pass(0, t)
+        round_w(1, 0, nc.scalar.copy)
+        invert_g(0, 0)
+        quantize_w(1, 0)
+        gather_tab(1)
+        for t in range(PACK):
+            first_pass(1, t)
+        for t in range(PACK):
+            magnitude(t)
+            divide_slice(t)
+            invert_g((t + 1) // PACK, (t + 1) % PACK)
+        invert_g(1, 1)
+        invert_g(1, 2)
+        gather_g(1, 3)
+        root_g(1, 3)
         first = [slice(0, 512), slice(512, 1024)]
         second = [slice(0, 256), slice(256, 512), slice(512, 768), slice(768, 896), slice(896, 1024)]
-        units = [(b, (first, second)[b][i]) for b, i in [(0,0),(0,1),(1,0),(1,1),(1,2),(1,3),(1,4)]]
-        for step in range(len(units) + 12):
-            for stage, lag in ((decay, 2), (invert, 0), (first_product, 0), (round_h, 3), (divide, 1), (quantize_h, 4), (second_product, 4), (copy_y, 5), (round_y, 6), (quantize_y, 7)):
-                if 0 <= step - lag < len(units):
-                    b, cols = units[step - lag]
+        square_g(1, 3)
+        decay(0, first[0])
+        round_w(0, 1, nc.vector.tensor_copy)
+        round_w(1, 1, nc.vector.tensor_copy)
+        quantize_w(0, 1)
+        quantize_w(1, 1)
+        for t in range(PACK):
+            signed_ratio(t, first[0])
+        round_h(0, first[0])
+        for t in range(PACK):
+            signed_ratio(t, first[1])
+        quantize_h(0, first[0])
+        stages = ((unsign, 0), (decay, 0), (round_h, 1), (quantize_h, 2), (second_product, 2), (copy_y, 3), (round_y, 4), (quantize_y, 5))
+        for step in range(len(second) + 5):
+            if step == 2:
+                decay(0, first[1])
+            for stage, lag in stages:
+                if 0 <= step - lag < len(second):
+                    cols = second[step - lag]
                     if stage in (second_product, copy_y, round_y, quantize_y):
-                        if b == 1:
-                            stage(cols)
-                    elif b == 1 or stage not in (invert, first_product):
-                        stage(b, cols)
+                        stage(cols)
+                    else:
+                        stage(1, cols)
+            if step == 2:
+                round_h(0, first[1])
+            if step == 3:
+                quantize_h(0, first[1])
         store_y_scales()

@@ -26,7 +26,7 @@ QUADS = 4
 ON_VECTOR = ()
 WINDOWS = 6
 WINDOW_BYTES = 4 * T
-ON_SCALAR = ()
+ON_SCALAR = (256,)
 SQUARES_ON_GPSIMD = ((0, 1), (0, 3))
 WORD_STORES = {768: 0, 1024: 768}
 
@@ -90,7 +90,9 @@ def tile_list_arrhenius_source_terms_kernel(
             w_raw[a, b] = raw
 
         def round_w(a, b, copy):
-            grouped = ring.tile([P, PASS * PACK], BF16, name="w_round", bufs=2, align_bytes=64)
+            grouped = hand.tile(
+                [P, PASS * PACK], BF16, name="w_round%d%d" % (a, b), offset=raw_at(2) + a * WINDOW_BYTES // 2, align_bytes=64
+            )
             copy(
                 grouped[:].rearrange("p (t m j) -> p m j t", t=PACK, j=PACK),
                 w_raw[a, b][:].rearrange("p j (m t) -> p m j t", t=PACK),
@@ -98,12 +100,15 @@ def tile_list_arrhenius_source_terms_kernel(
             w_round[a, b] = grouped
 
         def quantize_w(a, b):
-            codes = keep.tile([P, PASS], I32, name="w_codes%d%d" % (a, b), align_bytes=64)
+            if b == 0:
+                codes = hand.tile([P, PASS], I32, name="w_codes%d0" % a, offset=raw_at(4 + a), align_bytes=64)
+            else:
+                codes = keep.tile([P, PASS], I32, name="w_codes%d1" % a, align_bytes=64)
             scales = keep.tile([P, PASS], U8, name="w_scales%d%d" % (a, b), align_bytes=64)
             nc.vector.quantize_mx(codes[:].bitcast(FP8X4), scales[:], w_round[a, b][:])
             w_codes[a, b], w_scales[a, b] = codes, scales
 
-        tab = [keep.tile([P, T], I32, name="tab%d" % a) for a in range(2)]
+        tab = [hand.tile([P, T], I32, name="tab%d" % a, offset=raw_at(4 + a), align_bytes=64) for a in range(2)]
         picked = [keep.tile([P, S], I32, name="picked%d" % a, align_bytes=64) for a in range(2)]
         picked_plane = keep.tile([P, S], U8, name="picked_plane", align_bytes=64)
 
@@ -113,30 +118,37 @@ def tile_list_arrhenius_source_terms_kernel(
         def gather_tab(a):
             nc.vector.tensor_copy(picked[a][:].bitcast(U32), tab[a][:].bitcast(U32).indirect(offsets[:]))
 
-        signed = {}
+        unit_sums = {}
 
-        def signed_ratio(t, cols):
-            if cols.start not in signed:
-                signed[cols.start] = keep.tile([P, PACK, BANK], F32, name="signed%d" % cols.start)
-            acc = psum.tile([P, BANK], F32, name="acc")
-            m_cols = slice(t * P, (t + 1) * P)
-            for a in range(2):
+        def unit_pass(a, cols):
+            width = cols.stop - cols.start
+            per_bank = BANK // width
+            for t in range(PACK):
+                if a == 0 and t % per_bank == 0:
+                    unit_sums[cols.start, t // per_bank] = psum.tile([P, per_bank, width], F32, name="acc")
+                m_cols = slice(t * P, (t + 1) * P)
                 nc.tensor.matmul_mx(
-                    acc[:],
+                    unit_sums[cols.start, t // per_bank][:, t % per_bank, :],
                     lhsT=w_codes[a, 1][:, m_cols].bitcast(FP8X4),
                     lhsT_scale=w_scales[a, 1][:, m_cols],
                     rhs=picked[a][:, cols].bitcast(FP8X4),
                     rhs_scale=picked_plane[4 * a : P, cols],
-                    start=(a == 0),
-                    stop=(a == 1),
+                    start=(a == 0 and t % per_bank == 0),
+                    stop=(a == 1 and t % per_bank == per_bank - 1),
                 )
-            nc.vector.tensor_tensor(signed[cols.start][:, t, :], acc[:], temps[1][:, t, cols], ALU.mult)
 
-        def unsign(b, cols):
+        def signed_ratio(cols):
             width = cols.stop - cols.start
-            half = cols.start // BANK * BANK
-            pieces[b, cols.start] = keep.tile([P, PACK, width], F32, name="piece%d" % cols.start)
-            nc.scalar.activation(pieces[b, cols.start][:], signed[half][:, :, cols.start - half : cols.stop - half], ACT.Abs)
+            per_bank = BANK // width
+            pieces[1, cols.start] = keep.tile([P, PACK, width], F32, name="piece%d" % cols.start)
+            for bank in range(PACK // per_bank):
+                slices = slice(bank * per_bank, (bank + 1) * per_bank)
+                nc.vector.tensor_tensor(
+                    pieces[1, cols.start][:, slices, :], unit_sums[cols.start, bank][:], temps[1][:, slices, cols], ALU.mult
+                )
+
+        def unsign(cols):
+            nc.scalar.activation(pieces[1, cols.start][:], pieces[1, cols.start][:], ACT.Abs)
 
         sums = {}
 
@@ -167,40 +179,42 @@ def tile_list_arrhenius_source_terms_kernel(
 
         def decay(b, cols):
             if b == 0:
-                at = last - WINDOW_BYTES // 2 + 16 * cols.start
-                pieces[b, cols.start] = hand.tile([P, PACK, BANK], F32, name="decayed%d" % cols.start, offset=at, align_bytes=64)
+                at = last + cols.start // CHUNK % 2 * (WINDOW_BYTES // 2) + cols.start % CHUNK * 16
+                pieces[b, cols.start] = hand.tile(
+                    [P, PACK, cols.stop - cols.start], F32, name="decayed%d" % cols.start, offset=at, align_bytes=64
+                )
                 ratio = energy[0][:, :, cols]
             else:
                 ratio = pieces[b, cols.start][:]
             nc.scalar.activation(pieces[b, cols.start][:], ratio, ACT.Exp, scale=-1.0)
 
         factors = keep.tile([P, 2, PACK], F32, name="factors")
-        h_codes = [keep.tile([P, S], I32, name="h_codes%d" % b, align_bytes=64) for b in range(2)]
-        h_scales = [keep.tile([P, S], U8, name="h_scales%d" % b, align_bytes=64) for b in range(2)]
-        h_round = {}
+        h_round, h_codes, h_scales = {}, {}, {}
 
         def round_h(b, cols):
             width = cols.stop - cols.start
             if b == 0:
-                grouped = hand.tile(
-                    [P, width * PACK], BF16, name="h_round0_%d" % cols.start, offset=raw_at(1) + 8 * cols.start, align_bytes=64
+                at = {0: raw_at(2) + 7680, CHUNK: raw_at(2) + 512}.get(cols.start, raw_at(0) + cols.start * 16)
+                h_round[cols.start] = hand.tile(
+                    [P, 2, width * PACK], BF16, name="h_round%d" % cols.start, offset=at, align_bytes=64
                 )
-            else:
-                grouped = ring.tile([P, width * PACK], BF16, name="h_round", bufs=3, align_bytes=64)
             nc.vector.tensor_tensor(
-                grouped[:].rearrange("p (c i t) -> p c t i", i=2, t=PACK),
+                h_round[cols.start][:, b, :].rearrange("p (c i t) -> p c t i", i=2, t=PACK),
                 pieces[b, cols.start][:].rearrange("p t (c i) -> p c t i", i=2),
                 factors[:, b, :].unsqueeze(1).unsqueeze(3).to_broadcast([P, width // 2, PACK, 2]),
                 ALU.mult,
             )
-            h_round[b, cols.start] = grouped
 
-        def quantize_h(b, cols):
-            nc.vector.quantize_mx(h_codes[b][:, cols].bitcast(FP8X4), h_scales[b][:, cols], h_round[b, cols.start][:])
+        def quantize_h(cols):
+            width = cols.stop - cols.start
+            codes = keep.tile([P, 2 * width], I32, name="h_codes%d" % cols.start, align_bytes=64)
+            scales = keep.tile([P, 2 * width], U8, name="h_scales%d" % cols.start, align_bytes=64)
+            nc.vector.quantize_mx(codes[:].bitcast(FP8X4), scales[:], h_round[cols.start][:].rearrange("p b c -> p (b c)"))
+            h_codes[cols.start], h_scales[cols.start] = codes, scales
 
         wnu_raw = keep.tile([P, 2, 2 * N], U8, name="wnu_raw", align_bytes=64)
-        wnu_codes = keep.tile([P, 2, PACK, 2 * P], U8, name="wnu_codes", align_bytes=64)
-        wnu_plane = keep.tile([P, 2, PACK, P], U8, name="wnu_plane", align_bytes=64)
+        wnu_codes = hand.tile([P, 2, PACK, 2 * P], U8, name="wnu_codes", offset=raw_at(2) + 4608, align_bytes=64)
+        wnu_plane = hand.tile([P, 2, PACK, P], U8, name="wnu_plane", offset=raw_at(2) + 6656, align_bytes=64)
 
         def deal_wnu():
             nc.vector.tensor_copy(
@@ -217,15 +231,16 @@ def tile_list_arrhenius_source_terms_kernel(
         def second_product(cols):
             for c0 in range(cols.start, cols.stop, SUB):
                 banks[c0] = psum.tile([P, PACK, SUB], F32, name="acc")
-                sub = slice(c0, c0 + SUB)
                 for b in range(2):
+                    first_col = b * (cols.stop - cols.start) + c0 - cols.start
+                    sub = slice(first_col, first_col + SUB)
                     for t in range(PACK):
                         nc.tensor.matmul_mx(
                             banks[c0][:, t, :],
                             lhsT=wnu_codes[:, b, t, :].bitcast(FP4X4),
                             lhsT_scale=wnu_plane[:, b, t, :],
-                            rhs=h_codes[b][:, sub].bitcast(FP8X4),
-                            rhs_scale=h_scales[b][:, sub],
+                            rhs=h_codes[cols.start][:, sub].bitcast(FP8X4),
+                            rhs_scale=h_scales[cols.start][:, sub],
                             start=(b == 0 and t == 0),
                             stop=(b == 1 and t == PACK - 1),
                         )
@@ -296,41 +311,35 @@ def tile_list_arrhenius_source_terms_kernel(
                     out_2[0, 4 * q : 4 * q + 4, :].bitcast(I32), y_plane[32 * q : 32 * q + 4, :].bitcast(I32)
                 )
 
-        load_w(0, 0)
+        load_g(0, 0)
         load_tab_scales(nc.sync)
+        load_w(0, 0)
         load_tab(0)
+        load_w(1, 0)
+        load_tab(1)
+        for b, t in [(b, t) for b in range(2) for t in range(PACK)][1:]:
+            load_g(b, t)
+        load_w(0, 1)
+        load_w(1, 1)
         load_wnu_words(nc.sync)
         load_wnu_scales(nc.sync)
         load_factors(nc.sync)
-        load_w(1, 0)
-        load_g(0, 0)
-        load_tab(1)
-        load_g(0, 1)
-        load_g(0, 2)
-        load_g(0, 3)
-        load_g(1, 0)
-        load_g(1, 1)
-        load_g(1, 2)
-        load_g(1, 3)
-        load_w(0, 1)
-        load_w(1, 1)
 
         def invert_g(b, t):
             gather_g(b, t)
             root_g(b, t)
             square_g(b, t)
 
+        invert_g(0, 0)
         gather_tab_scales()
         round_w(0, 0, nc.scalar.copy)
         gather_tab(0)
         quantize_w(0, 0)
-        deal_wnu()
         for t in range(PACK):
             first_pass(0, t)
         round_w(1, 0, nc.scalar.copy)
-        invert_g(0, 0)
-        quantize_w(1, 0)
         gather_tab(1)
+        quantize_w(1, 0)
         for t in range(PACK):
             first_pass(1, t)
         for t in range(PACK):
@@ -341,33 +350,37 @@ def tile_list_arrhenius_source_terms_kernel(
         invert_g(1, 2)
         gather_g(1, 3)
         root_g(1, 3)
-        first = [slice(0, 512), slice(512, 1024)]
-        second = [slice(0, 256), slice(256, 512), slice(512, 768), slice(768, 896), slice(896, 1024)]
+        units = [slice(0, 256), slice(256, 512), slice(512, 768), slice(768, 896), slice(896, 1024)]
         square_g(1, 3)
-        decay(0, first[0])
         round_w(0, 1, nc.vector.tensor_copy)
         round_w(1, 1, nc.vector.tensor_copy)
         quantize_w(0, 1)
         quantize_w(1, 1)
-        for t in range(PACK):
-            signed_ratio(t, first[0])
-        round_h(0, first[0])
-        for t in range(PACK):
-            signed_ratio(t, first[1])
-        quantize_h(0, first[0])
-        stages = ((unsign, 0), (decay, 0), (round_h, 1), (quantize_h, 2), (second_product, 2), (copy_y, 3), (round_y, 4), (quantize_y, 5))
-        for step in range(len(second) + 5):
-            if step == 2:
-                decay(0, first[1])
+        deal_wnu()
+        for cols in units[:2]:
+            unit_pass(0, cols)
+
+        def ratio_unit(cols):
+            if cols not in units[:2]:
+                unit_pass(0, cols)
+            unit_pass(1, cols)
+            signed_ratio(cols)
+
+        stages = (
+            (copy_y, 4),
+            (lambda cols: decay(0, cols), 1),
+            (unsign, 1),
+            (lambda cols: decay(1, cols), 1),
+            (lambda cols: round_h(0, cols), 2),
+            (lambda cols: round_h(1, cols), 2),
+            (ratio_unit, 0),
+            (quantize_h, 2),
+            (second_product, 2),
+            (round_y, 6),
+            (quantize_y, 7),
+        )
+        for step in range(len(units) + 7):
             for stage, lag in stages:
-                if 0 <= step - lag < len(second):
-                    cols = second[step - lag]
-                    if stage in (second_product, copy_y, round_y, quantize_y):
-                        stage(cols)
-                    else:
-                        stage(1, cols)
-            if step == 2:
-                round_h(0, first[1])
-            if step == 3:
-                quantize_h(0, first[1])
+                if 0 <= step - lag < len(units):
+                    stage(units[step - lag])
         store_y_scales()

@@ -1,6 +1,7 @@
 from contextlib import ExitStack
 
 import concourse.mybir as mybir
+from concourse.masks import make_identity
 
 K, H, N, T, S = 1024, 1024, 512, 2048, 1024
 FLOPS = 2 * K * H * S + 2 * H * N * S
@@ -26,7 +27,8 @@ QUADS = 4
 ON_VECTOR = ()
 WINDOWS = 6
 WINDOW_BYTES = 4 * T
-ON_SCALAR = (256,)
+ON_SCALAR = ()
+ON_GPSIMD = (0, 256, 512)
 SQUARES_ON_GPSIMD = ((0, 1), (0, 3))
 WORD_STORES = {768: 0, 1024: 768}
 
@@ -41,7 +43,7 @@ def tile_list_arrhenius_source_terms_kernel(
         keep = ctx.enter_context(tc.tile_pool(name="keep", bufs=1))
         ring = ctx.enter_context(tc.tile_pool(name="ring", bufs=1))
         hand = ctx.enter_context(tc.tile_pool(name="hand", bufs=1))
-        psum = ctx.enter_context(tc.psum_pool(name="psum", bufs=8))
+        psum = ctx.enter_context(tc.psum_pool(name="psum", bufs=1))
 
         offsets = keep.tile([P, S // 16], U16, name="offsets")
         nc.sync.dma_start(offsets[:], offs)
@@ -57,6 +59,11 @@ def tile_list_arrhenius_source_terms_kernel(
         g_rows = gT.rearrange("(b p t) c -> b t p c", p=P, t=PACK)
 
         windows = {}
+        taken = []
+
+        def next_bank(count):
+            taken.append(count)
+            return "bank%d" % ((taken.count(count) - 1) % count)
 
         def window_at(b, t):
             return ((b * PACK + t) % WINDOWS) * WINDOW_BYTES
@@ -125,7 +132,7 @@ def tile_list_arrhenius_source_terms_kernel(
             per_bank = BANK // width
             for t in range(PACK):
                 if a == 0 and t % per_bank == 0:
-                    unit_sums[cols.start, t // per_bank] = psum.tile([P, per_bank, width], F32, name="acc")
+                    unit_sums[cols.start, t // per_bank] = psum.tile([P, per_bank, width], F32, name="acc", tag=next_bank(7))
                 m_cols = slice(t * P, (t + 1) * P)
                 nc.tensor.matmul_mx(
                     unit_sums[cols.start, t // per_bank][:, t % per_bank, :],
@@ -157,7 +164,7 @@ def tile_list_arrhenius_source_terms_kernel(
             for c0 in range(0, S, BANK):
                 cols = slice(c0, c0 + BANK)
                 if a == 0:
-                    sums[t, c0] = psum.tile([P, BANK], F32, name="acc")
+                    sums[t, c0] = psum.tile([P, BANK], F32, name="acc", tag=next_bank(8))
                 nc.tensor.matmul_mx(
                     sums[t, c0][:],
                     lhsT=w_codes[a, 0][:, m_cols].bitcast(FP8X4),
@@ -188,7 +195,16 @@ def tile_list_arrhenius_source_terms_kernel(
                 ratio = pieces[b, cols.start][:]
             nc.scalar.activation(pieces[b, cols.start][:], ratio, ACT.Exp, scale=-1.0)
 
-        factors = keep.tile([P, 2, PACK], F32, name="factors")
+        identity = keep.tile([P, P], F32, name="identity")
+        make_identity(nc, identity[:])
+        pre_rows = keep.tile([P, PASS], F32, name="pre_rows")
+        nc.gpsimd.memset(pre_rows[:], 0.0)
+        factors = psum.tile([P, PACK, P], F32, name="factors", tag="bank7")
+
+        def spread_factors():
+            for t in range(PACK):
+                nc.tensor.transpose(factors[:, t, :], pre_rows[:, t : PASS : PACK], identity[:])
+
         h_round, h_codes, h_scales = {}, {}, {}
 
         def round_h(b, cols):
@@ -201,7 +217,7 @@ def tile_list_arrhenius_source_terms_kernel(
             nc.vector.tensor_tensor(
                 h_round[cols.start][:, b, :].rearrange("p (c i t) -> p c t i", i=2, t=PACK),
                 pieces[b, cols.start][:].rearrange("p t (c i) -> p c t i", i=2),
-                factors[:, b, :].unsqueeze(1).unsqueeze(3).to_broadcast([P, width // 2, PACK, 2]),
+                factors[:, :, b].unsqueeze(1).unsqueeze(3).to_broadcast([P, width // 2, PACK, 2]),
                 ALU.mult,
             )
 
@@ -230,7 +246,7 @@ def tile_list_arrhenius_source_terms_kernel(
 
         def second_product(cols):
             for c0 in range(cols.start, cols.stop, SUB):
-                banks[c0] = psum.tile([P, PACK, SUB], F32, name="acc")
+                banks[c0] = psum.tile([P, PACK, SUB], F32, name="acc", tag=next_bank(7))
                 for b in range(2):
                     first_col = b * (cols.stop - cols.start) + c0 - cols.start
                     sub = slice(first_col, first_col + SUB)
@@ -262,12 +278,22 @@ def tile_list_arrhenius_source_terms_kernel(
 
         def round_y(cols):
             width = cols.stop - cols.start
-            grouped = ring.tile([P, width * PACK], BF16, name="y_round", bufs=2, align_bytes=64)
+            grouped = ring.tile([P, width * PACK], BF16, name="y_round", bufs=5, align_bytes=64)
             if cols.start in ON_SCALAR:
                 for c0 in range(0, width, SUB):
                     nc.scalar.copy(
                         grouped[:, c0 * PACK : (c0 + SUB) * PACK].rearrange("p (c t) -> p c t", t=PACK),
                         banks[cols.start + c0][:].rearrange("p t c -> p c t"),
+                    )
+            elif cols.start in ON_GPSIMD:
+                for c0 in range(0, width, SUB):
+                    nc.gpsimd.tensor_scalar(
+                        grouped[:, c0 * PACK : (c0 + SUB) * PACK].rearrange("p (c i t) -> p c t i", i=4, t=PACK),
+                        y_full[cols.start][:, :, c0 : c0 + SUB].rearrange("p t (c i) -> p c t i", i=4),
+                        1.0,
+                        0.0,
+                        ALU.mult,
+                        ALU.add,
                     )
             else:
                 nc.vector.tensor_copy(
@@ -300,7 +326,7 @@ def tile_list_arrhenius_source_terms_kernel(
                 )
 
         def load_factors(queue):
-            queue.dma_start(factors[:], pre.rearrange("(b p t) -> p b t", p=P, t=PACK))
+            queue.dma_start(pre_rows[0:2, :], pre.rearrange("(b c) -> b c", b=2))
 
         def gather_tab_scales():
             nc.vector.tensor_copy(picked_plane[:], tab_plane[:].indirect(offsets[:]))
@@ -317,13 +343,13 @@ def tile_list_arrhenius_source_terms_kernel(
         load_tab(0)
         load_w(1, 0)
         load_tab(1)
+        load_factors(nc.sync)
         for b, t in [(b, t) for b in range(2) for t in range(PACK)][1:]:
             load_g(b, t)
         load_w(0, 1)
         load_w(1, 1)
         load_wnu_words(nc.sync)
         load_wnu_scales(nc.sync)
-        load_factors(nc.sync)
 
         def invert_g(b, t):
             gather_g(b, t)
@@ -346,6 +372,7 @@ def tile_list_arrhenius_source_terms_kernel(
             magnitude(t)
             divide_slice(t)
             invert_g((t + 1) // PACK, (t + 1) % PACK)
+        spread_factors()
         invert_g(1, 1)
         invert_g(1, 2)
         gather_g(1, 3)
@@ -376,8 +403,8 @@ def tile_list_arrhenius_source_terms_kernel(
             (ratio_unit, 0),
             (quantize_h, 2),
             (second_product, 2),
-            (round_y, 6),
-            (quantize_y, 7),
+            (round_y, 4),
+            (quantize_y, 6),
         )
         for step in range(len(units) + 7):
             for stage, lag in stages:

@@ -205,19 +205,22 @@ def tile_list_arrhenius_source_terms_kernel(
             for t in range(PACK):
                 nc.tensor.transpose(factors[:, t, :], pre_rows[:, t : PASS : PACK], identity[:])
 
+        def h_round_at(start):
+            return {0: raw_at(2) + 7680, CHUNK: raw_at(2) + 512}.get(start, raw_at(0) + start * 16)
+
         h_round, h_codes, h_scales = {}, {}, {}
 
         def round_h(b, cols):
             width = cols.stop - cols.start
             if b == 0:
-                at = {0: raw_at(2) + 7680, CHUNK: raw_at(2) + 512}.get(cols.start, raw_at(0) + cols.start * 16)
+                at = h_round_at(cols.start)
                 h_round[cols.start] = hand.tile(
                     [P, 2, width * PACK], BF16, name="h_round%d" % cols.start, offset=at, align_bytes=64
                 )
             nc.vector.tensor_tensor(
-                h_round[cols.start][:, b, :].rearrange("p (c i t) -> p c t i", i=2, t=PACK),
-                pieces[b, cols.start][:].rearrange("p t (c i) -> p c t i", i=2),
-                factors[:, :, b].unsqueeze(1).unsqueeze(3).to_broadcast([P, width // 2, PACK, 2]),
+                h_round[cols.start][:, b, :].rearrange("p (c i t) -> p c t i", i=4, t=PACK),
+                pieces[b, cols.start][:].rearrange("p t (c i) -> p c t i", i=4),
+                factors[:, :, b].unsqueeze(1).unsqueeze(3).to_broadcast([P, width // 4, PACK, 4]),
                 ALU.mult,
             )
 
@@ -278,7 +281,12 @@ def tile_list_arrhenius_source_terms_kernel(
 
         def round_y(cols):
             width = cols.stop - cols.start
-            grouped = ring.tile([P, width * PACK], BF16, name="y_round", bufs=5, align_bytes=64)
+            if cols.start in ON_GPSIMD:
+                grouped = hand.tile(
+                    [P, width * PACK], BF16, name="y_round%d" % cols.start, offset=h_round_at(cols.stop), align_bytes=64
+                )
+            else:
+                grouped = ring.tile([P, width * PACK], BF16, name="y_round", bufs=2, align_bytes=64)
             if cols.start in ON_SCALAR:
                 for c0 in range(0, width, SUB):
                     nc.scalar.copy(
@@ -398,13 +406,13 @@ def tile_list_arrhenius_source_terms_kernel(
             (lambda cols: decay(0, cols), 1),
             (unsign, 1),
             (lambda cols: decay(1, cols), 1),
+            (round_y, 4),
             (lambda cols: round_h(0, cols), 2),
             (lambda cols: round_h(1, cols), 2),
             (ratio_unit, 0),
+            (quantize_y, 5),
             (quantize_h, 2),
             (second_product, 2),
-            (round_y, 4),
-            (quantize_y, 6),
         )
         for step in range(len(units) + 7):
             for stage, lag in stages:

@@ -80,13 +80,17 @@ def tile_list_arrhenius_source_terms_kernel(
             nc.vector.tensor_copy(temps[b][:, t, :], windows[b, t][:].indirect(offsets[:]))
 
         def root_g(b, t):
-            nc.scalar.activation(temps[b][:, t, :], temps[b][:, t, :], ACT.Abs_reciprocal_sqrt)
+            for c0 in range(0, S, BANK):
+                half = temps[b][:, t, c0 : c0 + BANK]
+                nc.scalar.activation(half, half, ACT.Abs_reciprocal_sqrt)
 
         def square_g(b, t):
             if (b, t) in SQUARES_ON_GPSIMD:
                 nc.gpsimd.tensor_tensor(temps[b][:, t, :], temps[b][:, t, :], temps[b][:, t, :], ALU.mult)
             else:
-                nc.scalar.activation(temps[b][:, t, :], temps[b][:, t, :], ACT.Square)
+                for c0 in range(0, S, BANK):
+                    half = temps[b][:, t, c0 : c0 + BANK]
+                    nc.scalar.activation(half, half, ACT.Square)
 
         w_raw, w_round, w_codes, w_scales = {}, {}, {}, {}
 
@@ -100,10 +104,11 @@ def tile_list_arrhenius_source_terms_kernel(
             grouped = hand.tile(
                 [P, PASS * PACK], BF16, name="w_round%d%d" % (a, b), offset=raw_at(2) + a * WINDOW_BYTES // 2, align_bytes=64
             )
-            copy(
-                grouped[:].rearrange("p (t m j) -> p m j t", t=PACK, j=PACK),
-                w_raw[a, b][:].rearrange("p j (m t) -> p m j t", t=PACK),
-            )
+            for pair in ([slice(0, PACK)], [slice(0, 2), slice(2, 4)])[b]:
+                copy(
+                    grouped[:].rearrange("p (t m j) -> p m j t", t=PACK, j=PACK)[:, :, :, pair],
+                    w_raw[a, b][:].rearrange("p j (m t) -> p m j t", t=PACK)[:, :, :, pair],
+                )
             w_round[a, b] = grouped
 
         def quantize_w(a, b):
@@ -112,7 +117,12 @@ def tile_list_arrhenius_source_terms_kernel(
             else:
                 codes = keep.tile([P, PASS], I32, name="w_codes%d1" % a, align_bytes=64)
             scales = keep.tile([P, PASS], U8, name="w_scales%d%d" % (a, b), align_bytes=64)
-            nc.vector.quantize_mx(codes[:].bitcast(FP8X4), scales[:], w_round[a, b][:])
+            part = PASS // (1 + b)
+            for c0 in range(0, PASS, part):
+                cols = slice(c0, c0 + part)
+                nc.vector.quantize_mx(
+                    codes[:, cols].bitcast(FP8X4), scales[:, cols], w_round[a, b][:, c0 * PACK : (c0 + part) * PACK]
+                )
             w_codes[a, b], w_scales[a, b] = codes, scales
 
         tab = [hand.tile([P, T], I32, name="tab%d" % a, offset=raw_at(4 + a), align_bytes=64) for a in range(2)]
@@ -403,8 +413,8 @@ def tile_list_arrhenius_source_terms_kernel(
 
         stages = (
             (copy_y, 4),
-            (lambda cols: decay(0, cols), 1),
             (unsign, 1),
+            (lambda cols: decay(0, cols), 1),
             (lambda cols: decay(1, cols), 1),
             (round_y, 4),
             (lambda cols: round_h(0, cols), 2),

@@ -306,8 +306,8 @@ def tile_list_arrhenius_source_terms_kernel(
             elif cols.start in ON_GPSIMD:
                 for c0 in range(0, width, SUB):
                     nc.gpsimd.tensor_scalar(
-                        grouped[:, c0 * PACK : (c0 + SUB) * PACK].rearrange("p (c i t) -> p c t i", i=4, t=PACK),
-                        y_full[cols.start][:, :, c0 : c0 + SUB].rearrange("p t (c i) -> p c t i", i=4),
+                        grouped[:, c0 * PACK : (c0 + SUB) * PACK].rearrange("p (c t) -> p c t", t=PACK),
+                        y_full[cols.start][:, :, c0 : c0 + SUB].rearrange("p t c -> p c t"),
                         1.0,
                         0.0,
                         ALU.mult,

@@ -24,11 +24,12 @@ BANK = 512
 CHUNK = 256
 SUB = 128
 QUADS = 4
-ON_VECTOR = ()
+ON_VECTOR = (384,)
 WINDOWS = 6
 WINDOW_BYTES = 4 * T
 ON_SCALAR = ()
 ON_GPSIMD = (0, 256, 512)
+H_ON_GPSIMD = (512,)
 SQUARES_ON_GPSIMD = ((0, 1), (0, 3))
 WORD_STORES = {768: 0, 1024: 768}
 
@@ -76,13 +77,16 @@ def tile_list_arrhenius_source_terms_kernel(
             nc.sync.dma_start(win[:], g_rows[b, t])
             windows[b, t] = win
 
+        def gathered(b, t):
+            return energy[0][:, t, :] if (b, t) in ((0, 1), (0, 2)) else temps[b][:, t, :]
+
         def gather_g(b, t):
-            nc.vector.tensor_copy(temps[b][:, t, :], windows[b, t][:].indirect(offsets[:]))
+            nc.vector.tensor_copy(gathered(b, t), windows[b, t][:].indirect(offsets[:]))
 
         def root_g(b, t):
             for c0 in range(0, S, BANK):
-                half = temps[b][:, t, c0 : c0 + BANK]
-                nc.scalar.activation(half, half, ACT.Abs_reciprocal_sqrt)
+                half = slice(c0, c0 + BANK)
+                nc.scalar.activation(temps[b][:, t, half], gathered(b, t)[:, half], ACT.Abs_reciprocal_sqrt)
 
         def square_g(b, t):
             if (b, t) in SQUARES_ON_GPSIMD:
@@ -100,11 +104,11 @@ def tile_list_arrhenius_source_terms_kernel(
             nc.sync.dma_start(raw[:], rows.rearrange("(p j) c -> p j c", j=PACK))
             w_raw[a, b] = raw
 
-        def round_w(a, b, copy):
+        def round_w(a, b, *copies):
             grouped = hand.tile(
                 [P, PASS * PACK], BF16, name="w_round%d%d" % (a, b), offset=raw_at(2) + a * WINDOW_BYTES // 2, align_bytes=64
             )
-            for pair in ([slice(0, PACK)], [slice(0, 2), slice(2, 4)])[b]:
+            for pair, copy in zip(([slice(0, PACK)], [slice(0, 2), slice(2, 4)])[len(copies) - 1], copies):
                 copy(
                     grouped[:].rearrange("p (t m j) -> p m j t", t=PACK, j=PACK)[:, :, :, pair],
                     w_raw[a, b][:].rearrange("p j (m t) -> p m j t", t=PACK)[:, :, :, pair],
@@ -112,10 +116,10 @@ def tile_list_arrhenius_source_terms_kernel(
             w_round[a, b] = grouped
 
         def quantize_w(a, b):
-            if b == 0:
+            if (a, b) == (0, 0):
                 codes = hand.tile([P, PASS], I32, name="w_codes%d0" % a, offset=raw_at(4 + a), align_bytes=64)
             else:
-                codes = keep.tile([P, PASS], I32, name="w_codes%d1" % a, align_bytes=64)
+                codes = keep.tile([P, PASS], I32, name="w_codes%d%d" % (a, b), align_bytes=64)
             scales = keep.tile([P, PASS], U8, name="w_scales%d%d" % (a, b), align_bytes=64)
             part = PASS // (1 + b)
             for c0 in range(0, PASS, part):
@@ -211,12 +215,15 @@ def tile_list_arrhenius_source_terms_kernel(
         nc.gpsimd.memset(pre_rows[:], 0.0)
         factors = psum.tile([P, PACK, P], F32, name="factors", tag="bank7")
 
+        factors_first = keep.tile([P, PACK], F32, name="factors_first")
+
         def spread_factors():
             for t in range(PACK):
                 nc.tensor.transpose(factors[:, t, :], pre_rows[:, t : PASS : PACK], identity[:])
+            nc.scalar.copy(factors_first[:], factors[:, :, 0])
 
         def h_round_at(start):
-            return {0: raw_at(2) + 7680, CHUNK: raw_at(2) + 512}.get(start, raw_at(0) + start * 16)
+            return {0: raw_at(2) + 7680, CHUNK: raw_at(2) + 512, 2 * CHUNK: raw_at(2) + 7680}.get(start, raw_at(0) + start * 16)
 
         h_round, h_codes, h_scales = {}, {}, {}
 
@@ -227,6 +234,14 @@ def tile_list_arrhenius_source_terms_kernel(
                 h_round[cols.start] = hand.tile(
                     [P, 2, width * PACK], BF16, name="h_round%d" % cols.start, offset=at, align_bytes=64
                 )
+            if b == 0 and cols.start in H_ON_GPSIMD:
+                nc.gpsimd.tensor_tensor(
+                    h_round[cols.start][:, b, :].rearrange("p (c i t) -> p c t i", i=4, t=PACK),
+                    pieces[b, cols.start][:].rearrange("p t (c i) -> p c t i", i=4),
+                    factors_first[:].unsqueeze(1).unsqueeze(3).to_broadcast([P, width // 4, PACK, 4]),
+                    ALU.mult,
+                )
+                return
             nc.vector.tensor_tensor(
                 h_round[cols.start][:, b, :].rearrange("p (c i t) -> p c t i", i=4, t=PACK),
                 pieces[b, cols.start][:].rearrange("p t (c i) -> p c t i", i=4),
@@ -306,8 +321,8 @@ def tile_list_arrhenius_source_terms_kernel(
             elif cols.start in ON_GPSIMD:
                 for c0 in range(0, width, SUB):
                     nc.gpsimd.tensor_scalar(
-                        grouped[:, c0 * PACK : (c0 + SUB) * PACK].rearrange("p (c t) -> p c t", t=PACK),
-                        y_full[cols.start][:, :, c0 : c0 + SUB].rearrange("p t c -> p c t"),
+                        grouped[:, c0 * PACK : (c0 + SUB) * PACK].rearrange("p (c i t) -> p c t i", i=4, t=PACK),
+                        y_full[cols.start][:, :, c0 : c0 + SUB].rearrange("p t (c i) -> p c t i", i=4),
                         1.0,
                         0.0,
                         ALU.mult,
@@ -381,9 +396,9 @@ def tile_list_arrhenius_source_terms_kernel(
         quantize_w(0, 0)
         for t in range(PACK):
             first_pass(0, t)
-        round_w(1, 0, nc.scalar.copy)
-        gather_tab(1)
+        round_w(1, 0, nc.scalar.copy, nc.vector.tensor_copy)
         quantize_w(1, 0)
+        gather_tab(1)
         for t in range(PACK):
             first_pass(1, t)
         for t in range(PACK):
@@ -397,8 +412,8 @@ def tile_list_arrhenius_source_terms_kernel(
         root_g(1, 3)
         units = [slice(0, 256), slice(256, 512), slice(512, 768), slice(768, 896), slice(896, 1024)]
         square_g(1, 3)
-        round_w(0, 1, nc.vector.tensor_copy)
-        round_w(1, 1, nc.vector.tensor_copy)
+        round_w(0, 1, nc.vector.tensor_copy, nc.vector.tensor_copy)
+        round_w(1, 1, nc.vector.tensor_copy, nc.vector.tensor_copy)
         quantize_w(0, 1)
         quantize_w(1, 1)
         deal_wnu()
@@ -416,11 +431,10 @@ def tile_list_arrhenius_source_terms_kernel(
             (unsign, 1),
             (lambda cols: decay(0, cols), 1),
             (lambda cols: decay(1, cols), 1),
-            (round_y, 4),
+            (lambda cols: round_y(cols) if cols.start in ON_GPSIMD else None, 4),
             (lambda cols: round_h(0, cols), 2),
             (lambda cols: round_h(1, cols), 2),
             (ratio_unit, 0),
-            (quantize_y, 5),
             (quantize_h, 2),
             (second_product, 2),
         )
@@ -428,4 +442,8 @@ def tile_list_arrhenius_source_terms_kernel(
             for stage, lag in stages:
                 if 0 <= step - lag < len(units):
                     stage(units[step - lag])
+        for cols in units:
+            if cols.start not in ON_GPSIMD:
+                round_y(cols)
+            quantize_y(cols)
         store_y_scales()

@@ -28,7 +28,7 @@ ON_VECTOR = (384,)
 WINDOWS = 6
 WINDOW_BYTES = 4 * T
 ON_SCALAR = ()
-ON_GPSIMD = (0, 256, 512)
+ON_GPSIMD = (0, 256)
 H_ON_GPSIMD = (512,)
 SQUARES_ON_GPSIMD = ((0, 1), (0, 3))
 WORD_STORES = {768: 0, 1024: 768}
@@ -311,7 +311,7 @@ def tile_list_arrhenius_source_terms_kernel(
                     [P, width * PACK], BF16, name="y_round%d" % cols.start, offset=h_round_at(cols.stop), align_bytes=64
                 )
             else:
-                grouped = ring.tile([P, width * PACK], BF16, name="y_round", bufs=2, align_bytes=64)
+                grouped = ring.tile([P, width * PACK], BF16, name="y_round", bufs=3, align_bytes=64)
             if cols.start in ON_SCALAR:
                 for c0 in range(0, width, SUB):
                     nc.scalar.copy(
@@ -442,8 +442,10 @@ def tile_list_arrhenius_source_terms_kernel(
             for stage, lag in stages:
                 if 0 <= step - lag < len(units):
                     stage(units[step - lag])
-        for cols in units:
-            if cols.start not in ON_GPSIMD:
-                round_y(cols)
+        for cols in units[2:4]:
+            round_y(cols)
+        for cols in units[:4]:
             quantize_y(cols)
+        round_y(units[4])
+        quantize_y(units[4])
         store_y_scales()

@@ -351,11 +351,11 @@ def tile_list_arrhenius_source_terms_kernel(
                     wnu_scales[:, 4 * q : 4 * q + 4, :].rearrange("a r c -> r a c").bitcast(I32),
                 )
 
-        def load_tab_scales(queue):
-            for q in range(QUADS):
-                queue.dma_start(
-                    tab_plane[32 * q : 32 * q + 8, :].bitcast(I32),
-                    tab_scales[:, 4 * q : 4 * q + 4, :].bitcast(I32),
+        def load_tab_scales(a):
+            for r in range(PACK):
+                nc.sync.dma_start(
+                    tab_plane[PACK * a + r : P : 32, :].bitcast(I32),
+                    tab_scales[a, r : 16 : PACK, :].bitcast(I32),
                 )
 
         def load_factors(queue):
@@ -371,9 +371,10 @@ def tile_list_arrhenius_source_terms_kernel(
                 )
 
         load_g(0, 0)
-        load_tab_scales(nc.sync)
-        load_w(0, 0)
+        load_tab_scales(0)
         load_tab(0)
+        load_tab_scales(1)
+        load_w(0, 0)
         load_w(1, 0)
         load_tab(1)
         load_factors(nc.sync)
@@ -390,9 +391,9 @@ def tile_list_arrhenius_source_terms_kernel(
             square_g(b, t)
 
         invert_g(0, 0)
+        gather_tab(0)
         gather_tab_scales()
         round_w(0, 0, nc.scalar.copy)
-        gather_tab(0)
         quantize_w(0, 0)
         for t in range(PACK):
             first_pass(0, t)

@@ -50,7 +50,8 @@ def tile_list_arrhenius_source_terms_kernel(
         nc.sync.dma_start(offsets[:], offs)
 
         tab_plane = keep.tile([P, T], U8, name="tab_plane", align_bytes=64)
-        wnu_plane_raw = keep.tile([P, 2, N], U8, name="wnu_plane_raw", align_bytes=64)
+        spare = (WINDOWS + 6) * WINDOW_BYTES
+        wnu_plane_raw = hand.tile([P, 2, N], U8, name="wnu_plane_raw", offset=spare, align_bytes=64)
         nc.vector.memset(tab_plane[:].bitcast(I32), 0)
         nc.vector.memset(wnu_plane_raw[:].bitcast(I32), 0)
 
@@ -88,9 +89,13 @@ def tile_list_arrhenius_source_terms_kernel(
                 half = slice(c0, c0 + BANK)
                 nc.scalar.activation(temps[b][:, t, half], gathered(b, t)[:, half], ACT.Abs_reciprocal_sqrt)
 
+        def early_columns(t):
+            return BANK if t == PACK - 1 else S
+
         def square_g(b, t):
             if (b, t) in SQUARES_ON_GPSIMD:
-                nc.gpsimd.tensor_tensor(temps[b][:, t, :], temps[b][:, t, :], temps[b][:, t, :], ALU.mult)
+                early = temps[b][:, t, : early_columns(t)]
+                nc.gpsimd.tensor_tensor(early, early, early, ALU.mult)
             else:
                 for c0 in range(0, S, BANK):
                     half = temps[b][:, t, c0 : c0 + BANK]
@@ -196,7 +201,14 @@ def tile_list_arrhenius_source_terms_kernel(
         last = window_at(1, PACK - 1)
 
         def divide_slice(t):
-            nc.gpsimd.tensor_tensor(energy[0][:, t, :], energy[0][:, t, :], temps[0][:, t, :], ALU.mult)
+            early = energy[0][:, t, : early_columns(t)]
+            nc.gpsimd.tensor_tensor(early, early, temps[0][:, t, : early_columns(t)], ALU.mult)
+
+        def late_half():
+            inverse = hand.tile([P, BANK], F32, name="late_inverse", offset=spare, align_bytes=64)
+            roots, rest = temps[0][:, PACK - 1, BANK:], energy[0][:, PACK - 1, BANK:]
+            nc.gpsimd.tensor_tensor(inverse[:], roots, roots, ALU.mult)
+            nc.gpsimd.tensor_tensor(rest, rest, inverse[:], ALU.mult)
 
         def decay(b, cols):
             if b == 0:
@@ -256,7 +268,7 @@ def tile_list_arrhenius_source_terms_kernel(
             nc.vector.quantize_mx(codes[:].bitcast(FP8X4), scales[:], h_round[cols.start][:].rearrange("p b c -> p (b c)"))
             h_codes[cols.start], h_scales[cols.start] = codes, scales
 
-        wnu_raw = keep.tile([P, 2, 2 * N], U8, name="wnu_raw", align_bytes=64)
+        wnu_raw = hand.tile([P, 2, 2 * N], U8, name="wnu_raw", offset=spare + 1024, align_bytes=64)
         wnu_codes = hand.tile([P, 2, PACK, 2 * P], U8, name="wnu_codes", offset=raw_at(2) + 4608, align_bytes=64)
         wnu_plane = hand.tile([P, 2, PACK, P], U8, name="wnu_plane", offset=raw_at(2) + 6656, align_bytes=64)
 
@@ -418,6 +430,7 @@ def tile_list_arrhenius_source_terms_kernel(
         quantize_w(0, 1)
         quantize_w(1, 1)
         deal_wnu()
+        late_half()
         for cols in units[:2]:
             unit_pass(0, cols)
 

@@ -21,98 +21,117 @@ P = 128
 PACK = 4
 PASS = P * PACK
 BANK = 512
-CHUNK = 256
 SUB = 128
 QUADS = 4
-ON_VECTOR = (384,)
-WINDOWS = 6
-WINDOW_BYTES = 4 * T
-ON_SCALAR = ()
-ON_GPSIMD = (0, 256)
-H_ON_GPSIMD = (512,)
-SQUARES_ON_GPSIMD = ((0, 1), (0, 3))
-WORD_STORES = {768: 0, 1024: 768}
+W = 4 * T
+UNITS = (slice(0, 256), slice(256, 512), slice(512, 768), slice(768, 896), slice(896, 1024))
+HALVES = (slice(0, BANK), slice(BANK, S))
+Y_COPY_ON_VECTOR = ()
+Y_ROUND_ON_GPSIMD = (0,)
+Y_ROUND_ON_SCALAR = (640, 896)
+WORD_STORES = {512: 0, 1024: 512}
 
 
 def tile_list_arrhenius_source_terms_kernel(
     tc, tab_words, tab_scales, offs, w1, gT, pre, wnu_words, wnu_scales, out_0, out_1, out_2
 ):
     nc = tc.nc
-    chunks = S // CHUNK
 
     with ExitStack() as ctx:
         keep = ctx.enter_context(tc.tile_pool(name="keep", bufs=1))
-        ring = ctx.enter_context(tc.tile_pool(name="ring", bufs=1))
         hand = ctx.enter_context(tc.tile_pool(name="hand", bufs=1))
         psum = ctx.enter_context(tc.psum_pool(name="psum", bufs=1))
+
+        def placed(shape, dtype, name, at):
+            return hand.tile(shape, dtype, name=name, offset=at, align_bytes=64)
+
+        def slot(i):
+            return i * W + (0, 1024, 1024)[i] if i < 3 else i * W + 3072
+
+        def bank(shape, number):
+            return psum.tile(shape, F32, name="acc", tag="bank%d" % number)
 
         offsets = keep.tile([P, S // 16], U16, name="offsets")
         nc.sync.dma_start(offsets[:], offs)
 
+        def listed(cols):
+            return offsets[:, cols.start // 16 : cols.stop // 16]
+
         tab_plane = keep.tile([P, T], U8, name="tab_plane", align_bytes=64)
-        spare = (WINDOWS + 6) * WINDOW_BYTES
-        wnu_plane_raw = hand.tile([P, 2, N], U8, name="wnu_plane_raw", offset=spare, align_bytes=64)
+        wnu_plane_raw = placed([P, 2, N], U8, "wnu_plane_raw", W)
+        wnu_raw = placed([P, 2, 2 * N], U8, "wnu_raw", slot(3) - 2048)
         nc.vector.memset(tab_plane[:].bitcast(I32), 0)
         nc.vector.memset(wnu_plane_raw[:].bitcast(I32), 0)
 
-        temps = [keep.tile([P, PACK, S], F32, name="temps%d" % b) for b in range(2)]
-        energy = [keep.tile([P, PACK, S], F32, name="energy0")]
-        pieces = {}
         g_rows = gT.rearrange("(b p t) c -> b t p c", p=P, t=PACK)
-
-        windows = {}
-        taken = []
-
-        def next_bank(count):
-            taken.append(count)
-            return "bank%d" % ((taken.count(count) - 1) % count)
-
-        def window_at(b, t):
-            return ((b * PACK + t) % WINDOWS) * WINDOW_BYTES
-
-        def raw_at(a):
-            return (WINDOWS + a) * WINDOW_BYTES
+        windows, w_raw = {}, {}
+        tab = [placed([P, T], I32, "tab%d" % a, slot(8 + a)) for a in range(2)]
+        pre_rows = keep.tile([P, PASS], F32, name="pre_rows")
+        identity = keep.tile([P, P], F32, name="identity")
+        make_identity(nc, identity[:])
+        nc.gpsimd.memset(pre_rows[:], 0.0)
 
         def load_g(b, t):
-            win = hand.tile([P, T], F32, name="g_window%d%d" % (b, t), offset=window_at(b, t), align_bytes=64)
-            nc.sync.dma_start(win[:], g_rows[b, t])
-            windows[b, t] = win
-
-        def gathered(b, t):
-            return energy[0][:, t, :] if (b, t) in ((0, 1), (0, 2)) else temps[b][:, t, :]
-
-        def gather_g(b, t):
-            nc.vector.tensor_copy(gathered(b, t), windows[b, t][:].indirect(offsets[:]))
-
-        def root_g(b, t):
-            for c0 in range(0, S, BANK):
-                half = slice(c0, c0 + BANK)
-                nc.scalar.activation(temps[b][:, t, half], gathered(b, t)[:, half], ACT.Abs_reciprocal_sqrt)
-
-        def early_columns(t):
-            return BANK if t == PACK - 1 else S
-
-        def square_g(b, t):
-            if (b, t) in SQUARES_ON_GPSIMD:
-                early = temps[b][:, t, : early_columns(t)]
-                nc.gpsimd.tensor_tensor(early, early, early, ALU.mult)
-            else:
-                for c0 in range(0, S, BANK):
-                    half = temps[b][:, t, c0 : c0 + BANK]
-                    nc.scalar.activation(half, half, ACT.Square)
-
-        w_raw, w_round, w_codes, w_scales = {}, {}, {}, {}
+            windows[b, t] = placed([P, T], F32, "g_window%d%d" % (b, t), slot(b * PACK + t))
+            nc.sync.dma_start(windows[b, t][:], g_rows[b, t])
 
         def load_w(a, b):
-            raw = hand.tile([P, PACK, PASS], F32, name="w_raw%d%d" % (a, b), offset=raw_at(a), align_bytes=64)
+            w_raw[a, b] = placed([P, PACK, PASS], F32, "w_raw%d%d" % (a, b), slot(10 + 2 * b + a))
             rows = w1[a * PASS : (a + 1) * PASS, b * PASS : (b + 1) * PASS]
-            nc.sync.dma_start(raw[:], rows.rearrange("(p j) c -> p j c", j=PACK))
-            w_raw[a, b] = raw
+            nc.sync.dma_start(w_raw[a, b][:], rows.rearrange("(p j) c -> p j c", j=PACK))
+
+        def load_tab(a):
+            nc.sync.dma_start(tab[a][:], tab_words[a].rearrange("p c i -> p (c i)").bitcast(I32))
+
+        def load_tab_scales(a):
+            for r in range(PACK):
+                nc.sync.dma_start(
+                    tab_plane[PACK * a + r : P : 32, :].bitcast(I32),
+                    tab_scales[a, r : 16 : PACK, :].bitcast(I32),
+                )
+
+        load_g(0, 0)
+        load_tab_scales(0)
+        load_tab(0)
+        load_tab_scales(1)
+        load_w(0, 0)
+        load_w(1, 0)
+        load_tab(1)
+        nc.sync.dma_start(pre_rows[0:2, :], pre.rearrange("(b c) -> b c", b=2))
+        for b, t in [(b, t) for b in range(2) for t in range(PACK)][1:]:
+            load_g(b, t)
+        load_w(0, 1)
+        load_w(1, 1)
+        nc.sync.dma_start(wnu_raw[:].bitcast(I32), wnu_words.rearrange("a p c -> p a c").bitcast(I32))
+        for q in range(QUADS):
+            nc.sync.dma_start(
+                wnu_plane_raw[32 * q : 32 * q + 4].bitcast(I32),
+                wnu_scales[:, 4 * q : 4 * q + 4, :].rearrange("a r c -> r a c").bitcast(I32),
+            )
+
+        inverse = [keep.tile([P, PACK, S], F32, name="inverse%d" % b) for b in range(2)]
+        energy = [keep.tile([P, PACK, S], F32, name="energy%d" % b) for b in range(2)]
+        gathered = {(b, t): inverse[b][:, t, :] for b in range(2) for t in range(PACK)}
+        roots = dict(gathered)
+
+        def gather_g(b, t, cols=slice(0, S)):
+            nc.vector.tensor_copy(gathered[b, t][:, cols], windows[b, t][:].indirect(listed(cols)))
+
+        def root_g(b, t, cols):
+            nc.scalar.activation(roots[b, t][:, cols], gathered[b, t][:, cols], ACT.Abs_reciprocal_sqrt)
+
+        def square_g(b, t, cols):
+            nc.scalar.activation(inverse[b][:, t, cols], roots[b, t][:, cols], ACT.Square)
+
+        def invert_g(b, t):
+            for step in (root_g, square_g):
+                for cols in HALVES:
+                    step(b, t, cols)
+
+        w_round, w_codes, w_scales = {}, {}, {}
 
         def round_w(a, b, *copies):
-            grouped = hand.tile(
-                [P, PASS * PACK], BF16, name="w_round%d%d" % (a, b), offset=raw_at(2) + a * WINDOW_BYTES // 2, align_bytes=64
-            )
+            grouped = placed([P, PASS * PACK], BF16, "w_round%d%d" % (a, b), slot(14) + a * W // 2)
             for pair, copy in zip(([slice(0, PACK)], [slice(0, 2), slice(2, 4)])[len(copies) - 1], copies):
                 copy(
                     grouped[:].rearrange("p (t m j) -> p m j t", t=PACK, j=PACK)[:, :, :, pair],
@@ -122,11 +141,11 @@ def tile_list_arrhenius_source_terms_kernel(
 
         def quantize_w(a, b):
             if (a, b) == (0, 0):
-                codes = hand.tile([P, PASS], I32, name="w_codes%d0" % a, offset=raw_at(4 + a), align_bytes=64)
+                codes = placed([P, PASS], I32, "w_codes00", slot(8))
             else:
                 codes = keep.tile([P, PASS], I32, name="w_codes%d%d" % (a, b), align_bytes=64)
             scales = keep.tile([P, PASS], U8, name="w_scales%d%d" % (a, b), align_bytes=64)
-            part = PASS // (1 + b)
+            part = PASS if (a, b) == (1, 0) else PASS // 2
             for c0 in range(0, PASS, part):
                 cols = slice(c0, c0 + part)
                 nc.vector.quantize_mx(
@@ -134,129 +153,173 @@ def tile_list_arrhenius_source_terms_kernel(
                 )
             w_codes[a, b], w_scales[a, b] = codes, scales
 
-        tab = [hand.tile([P, T], I32, name="tab%d" % a, offset=raw_at(4 + a), align_bytes=64) for a in range(2)]
         picked = [keep.tile([P, S], I32, name="picked%d" % a, align_bytes=64) for a in range(2)]
         picked_plane = keep.tile([P, S], U8, name="picked_plane", align_bytes=64)
 
-        def load_tab(a):
-            nc.sync.dma_start(tab[a][:], tab_words[a].rearrange("p c i -> p (c i)").bitcast(I32))
-
-        def gather_tab(a):
-            nc.vector.tensor_copy(picked[a][:].bitcast(U32), tab[a][:].bitcast(U32).indirect(offsets[:]))
-
-        unit_sums = {}
-
-        def unit_pass(a, cols):
-            width = cols.stop - cols.start
-            per_bank = BANK // width
-            for t in range(PACK):
-                if a == 0 and t % per_bank == 0:
-                    unit_sums[cols.start, t // per_bank] = psum.tile([P, per_bank, width], F32, name="acc", tag=next_bank(7))
-                m_cols = slice(t * P, (t + 1) * P)
-                nc.tensor.matmul_mx(
-                    unit_sums[cols.start, t // per_bank][:, t % per_bank, :],
-                    lhsT=w_codes[a, 1][:, m_cols].bitcast(FP8X4),
-                    lhsT_scale=w_scales[a, 1][:, m_cols],
-                    rhs=picked[a][:, cols].bitcast(FP8X4),
-                    rhs_scale=picked_plane[4 * a : P, cols],
-                    start=(a == 0 and t % per_bank == 0),
-                    stop=(a == 1 and t % per_bank == per_bank - 1),
-                )
-
-        def signed_ratio(cols):
-            width = cols.stop - cols.start
-            per_bank = BANK // width
-            pieces[1, cols.start] = keep.tile([P, PACK, width], F32, name="piece%d" % cols.start)
-            for bank in range(PACK // per_bank):
-                slices = slice(bank * per_bank, (bank + 1) * per_bank)
-                nc.vector.tensor_tensor(
-                    pieces[1, cols.start][:, slices, :], unit_sums[cols.start, bank][:], temps[1][:, slices, cols], ALU.mult
-                )
-
-        def unsign(cols):
-            nc.scalar.activation(pieces[1, cols.start][:], pieces[1, cols.start][:], ACT.Abs)
+        def gather_tab(a, cols):
+            nc.vector.tensor_copy(picked[a][:, cols].bitcast(U32), tab[a][:].bitcast(U32).indirect(listed(cols)))
 
         sums = {}
 
-        def first_pass(a, t):
+        def first_pass(a, b, t, cols, out, opens, closes):
             m_cols = slice(t * P, (t + 1) * P)
-            for c0 in range(0, S, BANK):
-                cols = slice(c0, c0 + BANK)
-                if a == 0:
-                    sums[t, c0] = psum.tile([P, BANK], F32, name="acc", tag=next_bank(8))
-                nc.tensor.matmul_mx(
-                    sums[t, c0][:],
-                    lhsT=w_codes[a, 0][:, m_cols].bitcast(FP8X4),
-                    lhsT_scale=w_scales[a, 0][:, m_cols],
-                    rhs=picked[a][:, cols].bitcast(FP8X4),
-                    rhs_scale=picked_plane[4 * a : P, cols],
-                    start=(a == 0),
-                    stop=(a == 1),
-                )
+            nc.tensor.matmul_mx(
+                out,
+                lhsT=w_codes[a, b][:, m_cols].bitcast(FP8X4),
+                lhsT_scale=w_scales[a, b][:, m_cols],
+                rhs=picked[a][:, cols].bitcast(FP8X4),
+                rhs_scale=picked_plane[4 * a : P, cols],
+                start=opens,
+                stop=closes,
+            )
 
-        def magnitude(t):
-            for c0 in range(0, S, BANK):
-                nc.scalar.activation(energy[0][:, t, c0 : c0 + BANK], sums[t, c0][:], ACT.Abs)
+        def row_pass(a, b, t, h):
+            if a == 0:
+                sums[b, t, h] = bank([P, BANK], 2 * t + h)
+            first_pass(a, b, t, HALVES[h], sums[b, t, h][:], a == 0, a == 1)
 
-        last = window_at(1, PACK - 1)
-
-        def divide_slice(t):
-            early = energy[0][:, t, : early_columns(t)]
-            nc.gpsimd.tensor_tensor(early, early, temps[0][:, t, : early_columns(t)], ALU.mult)
-
-        def late_half():
-            inverse = hand.tile([P, BANK], F32, name="late_inverse", offset=spare, align_bytes=64)
-            roots, rest = temps[0][:, PACK - 1, BANK:], energy[0][:, PACK - 1, BANK:]
-            nc.gpsimd.tensor_tensor(inverse[:], roots, roots, ALU.mult)
-            nc.gpsimd.tensor_tensor(rest, rest, inverse[:], ALU.mult)
-
-        def decay(b, cols):
-            if b == 0:
-                at = last + cols.start // CHUNK % 2 * (WINDOW_BYTES // 2) + cols.start % CHUNK * 16
-                pieces[b, cols.start] = hand.tile(
-                    [P, PACK, cols.stop - cols.start], F32, name="decayed%d" % cols.start, offset=at, align_bytes=64
-                )
-                ratio = energy[0][:, :, cols]
-            else:
-                ratio = pieces[b, cols.start][:]
-            nc.scalar.activation(pieces[b, cols.start][:], ratio, ACT.Exp, scale=-1.0)
-
-        identity = keep.tile([P, P], F32, name="identity")
-        make_identity(nc, identity[:])
-        pre_rows = keep.tile([P, PASS], F32, name="pre_rows")
-        nc.gpsimd.memset(pre_rows[:], 0.0)
-        factors = psum.tile([P, PACK, P], F32, name="factors", tag="bank7")
-
-        factors_first = keep.tile([P, PACK], F32, name="factors_first")
-
-        def spread_factors():
+        def quarter_pass(a, k):
+            cols = slice(256 * k, 256 * (k + 1))
             for t in range(PACK):
-                nc.tensor.transpose(factors[:, t, :], pre_rows[:, t : PASS : PACK], identity[:])
-            nc.scalar.copy(factors_first[:], factors[:, :, 0])
+                if a == 0 and t % 2 == 0:
+                    sums[k, t // 2] = bank([P, 2, 256], (2 * k + t // 2) % 6)
+                first_pass(a, 1, t, cols, sums[k, t // 2][:, t % 2, :], (a, t % 2) == (0, 0), (a, t % 2) == (1, 1))
 
-        def h_round_at(start):
-            return {0: raw_at(2) + 7680, CHUNK: raw_at(2) + 512, 2 * CHUNK: raw_at(2) + 7680}.get(start, raw_at(0) + start * 16)
+        def magnitude(b, t, h):
+            nc.scalar.activation(energy[b][:, t, HALVES[h]], sums[b, t, h][:], ACT.Abs)
 
-        h_round, h_codes, h_scales = {}, {}, {}
+        def divide(out, b, t, cols=slice(0, S)):
+            nc.gpsimd.tensor_tensor(out[:, cols], energy[b][:, t, cols], inverse[b][:, t, cols], ALU.mult)
+
+        gather_g(0, 0)
+        invert_g(0, 0)
+        gather_tab(0, slice(0, S))
+        nc.vector.tensor_copy(picked_plane[:], tab_plane[:].indirect(offsets[:]))
+        round_w(0, 0, nc.scalar.copy, nc.scalar.copy)
+        quantize_w(0, 0)
+        round_w(1, 0, nc.scalar.copy, nc.vector.tensor_copy)
+        quantize_w(1, 0)
+        for h in range(2):
+            gather_tab(1, HALVES[h])
+        for t0 in (0, 2):
+            for h in range(2):
+                for a in range(2):
+                    for t in (t0, t0 + 1):
+                        row_pass(a, 0, t, h)
+        for h in range(2):
+            magnitude(0, 0, h)
+            magnitude(0, 1, h)
+            divide(energy[0][:, 0, :], 0, 0, HALVES[h])
+        first, second = HALVES
+
+        def square_on_gpsimd(out, roots_of):
+            nc.gpsimd.tensor_tensor(out, roots_of, roots_of, ALU.mult)
+
+        magnitude(0, 2, 0)
+        gather_g(0, 1)
+        for cols in HALVES:
+            root_g(0, 1, cols)
+            square_on_gpsimd(inverse[0][:, 1, cols], roots[0, 1][:, cols])
+        divide(energy[0][:, 1, :], 0, 1)
+        magnitude(0, 2, 1)
+        magnitude(0, 3, 0)
+        magnitude(0, 3, 1)
+        factors = bank([P, PACK, P], 7)
+        for t in range(PACK):
+            nc.tensor.transpose(factors[:, t, :], pre_rows[:, t : PASS : PACK], identity[:])
+        gather_g(0, 2)
+        invert_g(0, 2)
+        divide(energy[0][:, 2, :], 0, 2)
+        gather_g(0, 3)
+        for cols in HALVES:
+            root_g(0, 3, cols)
+        square_on_gpsimd(inverse[0][:, 3, :], roots[0, 3])
+        divide(energy[0][:, 3, :], 0, 3)
+
+        for t in range(2):
+            gather_g(1, t)
+            invert_g(1, t)
+        spare_roots = keep.tile([P, 2, BANK], F32, name="spare_roots")
+        gathered[1, 3] = placed([P, S], F32, "gathered13", slot(8))[:]
+        gather_g(1, 2)
+        for cols in HALVES:
+            gather_g(1, 3, cols)
+        root_g(1, 2, first)
+        nc.scalar.activation(spare_roots[:, 0, :], gathered[1, 2][:, second], ACT.Abs_reciprocal_sqrt)
+        roots[1, 3] = spare_roots[:, 1, :]
+        root_g(1, 3, first)
+        square_on_gpsimd(inverse[1][:, 2, first], roots[1, 2][:, first])
+        square_g(1, 3, first)
+        nc.scalar.activation(spare_roots[:, 1, :], gathered[1, 3][:, second], ACT.Abs_reciprocal_sqrt)
+        for a in range(2):
+            round_w(a, 1, nc.vector.tensor_copy, nc.vector.tensor_copy)
+            quantize_w(a, 1)
+
+        wnu_codes = placed([P, 2, PACK, 2 * P], U8, "wnu_codes", slot(14))
+        wnu_plane = placed([P, 2, PACK, P], U8, "wnu_plane", slot(14) + 2048)
+        nc.vector.tensor_copy(
+            wnu_codes[:].bitcast(U16).rearrange("p a t m -> p a m t"),
+            wnu_raw[:].bitcast(U16).rearrange("p a (m t) -> p a m t", t=PACK),
+        )
+        nc.vector.tensor_copy(
+            wnu_plane[:].rearrange("p a t m -> p a m t"),
+            wnu_plane_raw[:].rearrange("p a (m t) -> p a m t", t=PACK),
+        )
+        late_inverse = placed([P, 2, BANK], F32, "late_inverse", W // 2 + 64)
+        square_on_gpsimd(late_inverse[:], spare_roots[:])
+        for k in range(3):
+            quarter_pass(0, k)
+        for k in range(3):
+            quarter_pass(1, k)
+
+        def signed_ratio(k):
+            cols = slice(256 * k, 256 * (k + 1))
+            for i in range(2):
+                pair = slice(2 * i, 2 * i + 2)
+                nc.vector.tensor_tensor(energy[1][:, pair, cols], sums[k, i][:], inverse[1][:, pair, cols], ALU.mult)
+
+        def late_magnitude(k, i):
+            nc.scalar.activation(energy[1][:, 2 * i : 2 * i + 2, 256 * k : 256 * (k + 1)], sums[k, i][:], ACT.Abs)
+
+        def late_ratio(out, k, i):
+            cols = slice(256 * k, 256 * (k + 1))
+            by = late_inverse[:, :, 256 * k - BANK : 256 * k - 256] if i else inverse[1][:, 0:2, cols]
+            nc.gpsimd.tensor_tensor(out, energy[1][:, 2 * i : 2 * i + 2, cols], by, ALU.mult)
+
+        decayed, h_round, h_codes, h_scales, y_sums, y_full, y_round = {}, {}, {}, {}, {}, {}, {}
+        decayed0_at = {0: slot(8), 256: slot(12), 512: slot(12) + W // 2, 768: slot(8)}
+        h_round_at = {0: slot(1) - 64, 256: slot(3) - 6080, 512: slot(3) - 64, 768: 0, 896: 2048}
+        y_round_at = {0: h_round_at[512], 256: slot(12) - 4032, 512: slot(12) - 1984, 768: slot(9), 896: slot(9) + 1024}
+
+        def share(b, cols, out):
+            for unit in UNITS:
+                if cols.start <= unit.start < cols.stop:
+                    decayed[b, unit.start] = out[:, :, unit.start - cols.start : unit.stop - cols.start]
+
+        def decay0(cols):
+            out = placed([P, PACK, cols.stop - cols.start], F32, "decayed0_%d" % cols.start, decayed0_at[cols.start])
+            nc.scalar.activation(out[:], energy[0][:, :, cols], ACT.Exp, scale=-1.0)
+            share(0, cols, out)
+
+        def unsign(cols):
+            nc.scalar.activation(energy[1][:, :, cols], energy[1][:, :, cols], ACT.Abs)
+
+        def decay1(cols):
+            out = placed([P, PACK, cols.stop - cols.start], F32, "decayed1_%d" % cols.start, slot(10) + cols.start * 16)
+            if cols.stop < S:
+                nc.scalar.activation(out[:], energy[1][:, :, cols], ACT.Exp, scale=-1.0)
+            else:
+                nc.scalar.activation(out[:, 0:2, :], energy[1][:, 0:2, cols], ACT.Exp, scale=-1.0)
+                nc.scalar.activation(out[:, 2:4, :], last_ratio[:], ACT.Exp, scale=-1.0)
+            share(1, cols, out)
 
         def round_h(b, cols):
             width = cols.stop - cols.start
             if b == 0:
-                at = h_round_at(cols.start)
-                h_round[cols.start] = hand.tile(
-                    [P, 2, width * PACK], BF16, name="h_round%d" % cols.start, offset=at, align_bytes=64
-                )
-            if b == 0 and cols.start in H_ON_GPSIMD:
-                nc.gpsimd.tensor_tensor(
-                    h_round[cols.start][:, b, :].rearrange("p (c i t) -> p c t i", i=4, t=PACK),
-                    pieces[b, cols.start][:].rearrange("p t (c i) -> p c t i", i=4),
-                    factors_first[:].unsqueeze(1).unsqueeze(3).to_broadcast([P, width // 4, PACK, 4]),
-                    ALU.mult,
-                )
-                return
+                h_round[cols.start] = placed([P, 2, width * PACK], BF16, "h_round%d" % cols.start, h_round_at[cols.start])
             nc.vector.tensor_tensor(
                 h_round[cols.start][:, b, :].rearrange("p (c i t) -> p c t i", i=4, t=PACK),
-                pieces[b, cols.start][:].rearrange("p t (c i) -> p c t i", i=4),
+                decayed[b, cols.start].rearrange("p t (c i) -> p c t i", i=4),
                 factors[:, :, b].unsqueeze(1).unsqueeze(3).to_broadcast([P, width // 4, PACK, 4]),
                 ALU.mult,
             )
@@ -268,31 +331,15 @@ def tile_list_arrhenius_source_terms_kernel(
             nc.vector.quantize_mx(codes[:].bitcast(FP8X4), scales[:], h_round[cols.start][:].rearrange("p b c -> p (b c)"))
             h_codes[cols.start], h_scales[cols.start] = codes, scales
 
-        wnu_raw = hand.tile([P, 2, 2 * N], U8, name="wnu_raw", offset=spare + 1024, align_bytes=64)
-        wnu_codes = hand.tile([P, 2, PACK, 2 * P], U8, name="wnu_codes", offset=raw_at(2) + 4608, align_bytes=64)
-        wnu_plane = hand.tile([P, 2, PACK, P], U8, name="wnu_plane", offset=raw_at(2) + 6656, align_bytes=64)
-
-        def deal_wnu():
-            nc.vector.tensor_copy(
-                wnu_codes[:].bitcast(U16).rearrange("p a t m -> p a m t"),
-                wnu_raw[:].bitcast(U16).rearrange("p a (m t) -> p a m t", t=PACK),
-            )
-            nc.vector.tensor_copy(
-                wnu_plane[:].rearrange("p a t m -> p a m t"),
-                wnu_plane_raw[:].rearrange("p a (m t) -> p a m t", t=PACK),
-            )
-
-        banks = {}
-
         def second_product(cols):
             for c0 in range(cols.start, cols.stop, SUB):
-                banks[c0] = psum.tile([P, PACK, SUB], F32, name="acc", tag=next_bank(7))
+                y_sums[c0] = bank([P, PACK, SUB], (6 + c0 // SUB) % 7)
                 for b in range(2):
                     first_col = b * (cols.stop - cols.start) + c0 - cols.start
                     sub = slice(first_col, first_col + SUB)
                     for t in range(PACK):
                         nc.tensor.matmul_mx(
-                            banks[c0][:, t, :],
+                            y_sums[c0][:, t, :],
                             lhsT=wnu_codes[:, b, t, :].bitcast(FP4X4),
                             lhsT_scale=wnu_plane[:, b, t, :],
                             rhs=h_codes[cols.start][:, sub].bitcast(FP8X4),
@@ -303,34 +350,22 @@ def tile_list_arrhenius_source_terms_kernel(
 
         y_rows = out_0.rearrange("(p t) c -> p t c", t=PACK)
         y_words = out_1[0].rearrange("p c t -> p (c t)").bitcast(I32)
-        y_plane = keep.tile([P, S], U8, name="y_plane", align_bytes=64)
+        y_plane = placed([P, S], U8, "y_plane", h_round_at[896])
         y_codes = keep.tile([P, S], I32, name="y_codes", align_bytes=64)
-        y_full, y_round = {}, {}
 
         def copy_y(cols):
             width = cols.stop - cols.start
-            y = keep.tile([P, PACK, width], F32, name="y%d" % cols.start)[:]
+            y = placed([P, PACK, width], F32, "y%d" % cols.start, slot(4) + cols.start * 16)[:]
             for c0 in range(0, width, SUB):
-                copy = nc.vector.tensor_copy if cols.start + c0 in ON_VECTOR else nc.scalar.copy
-                copy(y[:, :, c0 : c0 + SUB], banks[cols.start + c0][:])
+                copy = nc.vector.tensor_copy if cols.start + c0 in Y_COPY_ON_VECTOR else nc.scalar.copy
+                copy(y[:, :, c0 : c0 + SUB], y_sums[cols.start + c0][:])
             nc.sync.dma_start(y_rows[:, :, cols], y)
             y_full[cols.start] = y
 
         def round_y(cols):
             width = cols.stop - cols.start
-            if cols.start in ON_GPSIMD:
-                grouped = hand.tile(
-                    [P, width * PACK], BF16, name="y_round%d" % cols.start, offset=h_round_at(cols.stop), align_bytes=64
-                )
-            else:
-                grouped = ring.tile([P, width * PACK], BF16, name="y_round", bufs=3, align_bytes=64)
-            if cols.start in ON_SCALAR:
-                for c0 in range(0, width, SUB):
-                    nc.scalar.copy(
-                        grouped[:, c0 * PACK : (c0 + SUB) * PACK].rearrange("p (c t) -> p c t", t=PACK),
-                        banks[cols.start + c0][:].rearrange("p t c -> p c t"),
-                    )
-            elif cols.start in ON_GPSIMD:
+            grouped = placed([P, width * PACK], BF16, "y_round%d" % cols.start, y_round_at[cols.start])
+            if cols.start in Y_ROUND_ON_GPSIMD:
                 for c0 in range(0, width, SUB):
                     nc.gpsimd.tensor_scalar(
                         grouped[:, c0 * PACK : (c0 + SUB) * PACK].rearrange("p (c i t) -> p c t i", i=4, t=PACK),
@@ -341,10 +376,17 @@ def tile_list_arrhenius_source_terms_kernel(
                         ALU.add,
                     )
             else:
-                nc.vector.tensor_copy(
-                    grouped[:].rearrange("p (c i t) -> p c t i", i=4, t=PACK),
-                    y_full[cols.start].rearrange("p t (c i) -> p c t i", i=4),
-                )
+                own = width - SUB * (cols.stop - SUB in Y_ROUND_ON_SCALAR)
+                if own:
+                    nc.vector.tensor_copy(
+                        grouped[:, : own * PACK].rearrange("p (c i t) -> p c t i", i=4, t=PACK),
+                        y_full[cols.start][:, :, :own].rearrange("p t (c i) -> p c t i", i=4),
+                    )
+                if own < width:
+                    nc.scalar.copy(
+                        grouped[:, own * PACK :].rearrange("p (c t) -> p c t", t=PACK),
+                        y_sums[cols.stop - SUB][:].rearrange("p t c -> p c t"),
+                    )
             y_round[cols.start] = grouped
 
         def quantize_y(cols):
@@ -353,113 +395,61 @@ def tile_list_arrhenius_source_terms_kernel(
                 done = slice(WORD_STORES[cols.stop], cols.stop)
                 nc.sync.dma_start(y_words[:, done], y_codes[:, done])
 
-        def load_wnu_words(queue):
-            queue.dma_start(wnu_raw[:].bitcast(I32), wnu_words.rearrange("a p c -> p a c").bitcast(I32))
+        def source_terms(cols):
+            quantize_h(cols)
+            second_product(cols)
 
-        def load_wnu_scales(queue):
-            for q in range(QUADS):
-                queue.dma_start(
-                    wnu_plane_raw[32 * q : 32 * q + 4].bitcast(I32),
-                    wnu_scales[:, 4 * q : 4 * q + 4, :].rearrange("a r c -> r a c").bitcast(I32),
-                )
-
-        def load_tab_scales(a):
-            for r in range(PACK):
-                nc.sync.dma_start(
-                    tab_plane[PACK * a + r : P : 32, :].bitcast(I32),
-                    tab_scales[a, r : 16 : PACK, :].bitcast(I32),
-                )
-
-        def load_factors(queue):
-            queue.dma_start(pre_rows[0:2, :], pre.rearrange("(b c) -> b c", b=2))
-
-        def gather_tab_scales():
-            nc.vector.tensor_copy(picked_plane[:], tab_plane[:].indirect(offsets[:]))
-
-        def store_y_scales():
-            for q in range(QUADS):
-                nc.sync.dma_start(
-                    out_2[0, 4 * q : 4 * q + 4, :].bitcast(I32), y_plane[32 * q : 32 * q + 4, :].bitcast(I32)
-                )
-
-        load_g(0, 0)
-        load_tab_scales(0)
-        load_tab(0)
-        load_tab_scales(1)
-        load_w(0, 0)
-        load_w(1, 0)
-        load_tab(1)
-        load_factors(nc.sync)
-        for b, t in [(b, t) for b in range(2) for t in range(PACK)][1:]:
-            load_g(b, t)
-        load_w(0, 1)
-        load_w(1, 1)
-        load_wnu_words(nc.sync)
-        load_wnu_scales(nc.sync)
-
-        def invert_g(b, t):
-            gather_g(b, t)
-            root_g(b, t)
-            square_g(b, t)
-
-        invert_g(0, 0)
-        gather_tab(0)
-        gather_tab_scales()
-        round_w(0, 0, nc.scalar.copy)
-        quantize_w(0, 0)
-        for t in range(PACK):
-            first_pass(0, t)
-        round_w(1, 0, nc.scalar.copy, nc.vector.tensor_copy)
-        quantize_w(1, 0)
-        gather_tab(1)
-        for t in range(PACK):
-            first_pass(1, t)
-        for t in range(PACK):
-            magnitude(t)
-            divide_slice(t)
-            invert_g((t + 1) // PACK, (t + 1) % PACK)
-        spread_factors()
-        invert_g(1, 1)
-        invert_g(1, 2)
-        gather_g(1, 3)
-        root_g(1, 3)
-        units = [slice(0, 256), slice(256, 512), slice(512, 768), slice(768, 896), slice(896, 1024)]
-        square_g(1, 3)
-        round_w(0, 1, nc.vector.tensor_copy, nc.vector.tensor_copy)
-        round_w(1, 1, nc.vector.tensor_copy, nc.vector.tensor_copy)
-        quantize_w(0, 1)
-        quantize_w(1, 1)
-        deal_wnu()
-        late_half()
-        for cols in units[:2]:
-            unit_pass(0, cols)
-
-        def ratio_unit(cols):
-            if cols not in units[:2]:
-                unit_pass(0, cols)
-            unit_pass(1, cols)
-            signed_ratio(cols)
-
-        stages = (
-            (copy_y, 4),
-            (unsign, 1),
-            (lambda cols: decay(0, cols), 1),
-            (lambda cols: decay(1, cols), 1),
-            (lambda cols: round_y(cols) if cols.start in ON_GPSIMD else None, 4),
-            (lambda cols: round_h(0, cols), 2),
-            (lambda cols: round_h(1, cols), 2),
-            (ratio_unit, 0),
-            (quantize_h, 2),
-            (second_product, 2),
-        )
-        for step in range(len(units) + 7):
-            for stage, lag in stages:
-                if 0 <= step - lag < len(units):
-                    stage(units[step - lag])
-        for cols in units[2:4]:
-            round_y(cols)
-        for cols in units[:4]:
-            quantize_y(cols)
-        round_y(units[4])
-        quantize_y(units[4])
-        store_y_scales()
+        u0, u1, u2, u3, u4 = UNITS
+        for cols in (u0, u1, u2):
+            decay0(cols)
+        signed_ratio(0)
+        for a in range(2):
+            quarter_pass(a, 3)
+        signed_ratio(1)
+        round_h(0, u0)
+        round_h(0, u1)
+        for i in range(2):
+            late_magnitude(2, i)
+            late_ratio(energy[1][:, 2 * i : 2 * i + 2, u2], 2, i)
+        unsign(u0)
+        decay1(u0)
+        unsign(u1)
+        round_h(0, u2)
+        round_h(1, u0)
+        source_terms(u0)
+        last = slice(u3.start, u4.stop)
+        last_ratio = placed([P, 2, 256], F32, "last_ratio", h_round_at[u0.start])
+        decay1(u1)
+        for i, out in enumerate((energy[1][:, 0:2, last], last_ratio[:])):
+            late_magnitude(3, i)
+            late_ratio(out, 3, i)
+        round_h(1, u1)
+        source_terms(u1)
+        decay1(u2)
+        decay0(last)
+        round_h(1, u2)
+        source_terms(u2)
+        round_h(0, u3)
+        copy_y(u0)
+        round_y(u0)
+        decay1(last)
+        round_h(0, u4)
+        round_h(1, u3)
+        round_h(1, u4)
+        source_terms(u3)
+        source_terms(u4)
+        copy_y(u1)
+        copy_y(u2)
+        quantize_y(u0)
+        round_y(u1)
+        round_y(u2)
+        copy_y(u3)
+        copy_y(u4)
+        quantize_y(u1)
+        quantize_y(u2)
+        round_y(u3)
+        round_y(u4)
+        quantize_y(u3)
+        quantize_y(u4)
+        for q in range(QUADS):
+            nc.sync.dma_start(out_2[0, 4 * q : 4 * q + 4, :].bitcast(I32), y_plane[32 * q : 32 * q + 4, :].bitcast(I32))

@@ -29,6 +29,7 @@ HALVES = (slice(0, BANK), slice(BANK, S))
 Y_COPY_ON_VECTOR = ()
 Y_ROUND_ON_GPSIMD = (0,)
 Y_ROUND_ON_SCALAR = (640, 896)
+STORED_BY_BANK = (0, 256)
 WORD_STORES = {512: 0, 1024: 512}
 
 
@@ -359,8 +360,13 @@ def tile_list_arrhenius_source_terms_kernel(
             for c0 in range(0, width, SUB):
                 copy = nc.vector.tensor_copy if cols.start + c0 in Y_COPY_ON_VECTOR else nc.scalar.copy
                 copy(y[:, :, c0 : c0 + SUB], y_sums[cols.start + c0][:])
-            nc.sync.dma_start(y_rows[:, :, cols], y)
-            y_full[cols.start] = y
+                if cols.start in STORED_BY_BANK:
+                    nc.sync.dma_start(y_rows[:, :, cols.start + c0 : cols.start + c0 + SUB], y[:, :, c0 : c0 + SUB])
+            if cols.start not in STORED_BY_BANK:
+                nc.sync.dma_start(y_rows[:, :, cols], y)
+            for unit in UNITS:
+                if cols.start <= unit.start < cols.stop:
+                    y_full[unit.start] = y[:, :, unit.start - cols.start : unit.stop - cols.start]
 
         def round_y(cols):
             width = cols.stop - cols.start
@@ -443,8 +449,7 @@ def tile_list_arrhenius_source_terms_kernel(
         quantize_y(u0)
         round_y(u1)
         round_y(u2)
-        copy_y(u3)
-        copy_y(u4)
+        copy_y(last)
         quantize_y(u1)
         quantize_y(u2)
         round_y(u3)

@@ -372,7 +372,7 @@ def tile_list_arrhenius_source_terms_kernel(
             width = cols.stop - cols.start
             grouped = placed([P, width * PACK], BF16, "y_round%d" % cols.start, y_round_at[cols.start])
             if cols.start in Y_ROUND_ON_GPSIMD:
-                for c0 in range(0, width, SUB):
+                for c0 in range(0, SUB, SUB):
                     nc.gpsimd.tensor_scalar(
                         grouped[:, c0 * PACK : (c0 + SUB) * PACK].rearrange("p (c i t) -> p c t i", i=4, t=PACK),
                         y_full[cols.start][:, :, c0 : c0 + SUB].rearrange("p t (c i) -> p c t i", i=4),
@@ -446,8 +446,12 @@ def tile_list_arrhenius_source_terms_kernel(
         source_terms(u4)
         copy_y(u1)
         copy_y(u2)
-        quantize_y(u0)
+        nc.vector.tensor_copy(
+            y_round[0][:, SUB * PACK :].rearrange("p (c i t) -> p c t i", i=4, t=PACK),
+            y_full[0][:, :, SUB:].rearrange("p t (c i) -> p c t i", i=4),
+        )
         round_y(u1)
+        quantize_y(u0)
         round_y(u2)
         copy_y(last)
         quantize_y(u1)

@@ -29,8 +29,8 @@ HALVES = (slice(0, BANK), slice(BANK, S))
 Y_COPY_ON_VECTOR = ()
 Y_ROUND_ON_GPSIMD = (0,)
 Y_ROUND_ON_SCALAR = (640, 896)
-STORED_BY_BANK = (0, 256)
-WORD_STORES = {512: 0, 1024: 512}
+STORED_BY_BANK = ()
+WORD_STORES = {1024: 0}
 
 
 def tile_list_arrhenius_source_terms_kernel(
@@ -53,7 +53,6 @@ def tile_list_arrhenius_source_terms_kernel(
             return psum.tile(shape, F32, name="acc", tag="bank%d" % number)
 
         offsets = keep.tile([P, S // 16], U16, name="offsets")
-        nc.sync.dma_start(offsets[:], offs)
 
         def listed(cols):
             return offsets[:, cols.start // 16 : cols.stop // 16]
@@ -92,6 +91,7 @@ def tile_list_arrhenius_source_terms_kernel(
                 )
 
         load_g(0, 0)
+        nc.sync.dma_start(offsets[:], offs)
         load_tab_scales(0)
         load_tab(0)
         load_tab_scales(1)

from contextlib import ExitStack

import concourse.mybir as mybir
from concourse.masks import make_identity

K, H, N, T, S = 1024, 1024, 512, 2048, 1024
FLOPS = 2 * K * H * S + 2 * H * N * S

F32 = mybir.dt.float32
BF16 = mybir.dt.bfloat16
I32 = mybir.dt.int32
U32 = mybir.dt.uint32
U16 = mybir.dt.uint16
U8 = mybir.dt.uint8
FP8X4 = mybir.dt.float8_e4m3fn_x4
FP4X4 = mybir.dt.float4_e2m1fn_x4
ACT = mybir.ActivationFunctionType
ALU = mybir.AluOpType

P = 128
PACK = 4
PASS = P * PACK
BANK = 512
SUB = 128
QUADS = 4
W = 4 * T
UNITS = (slice(0, 256), slice(256, 512), slice(512, 768), slice(768, 896), slice(896, 1024))
HALVES = (slice(0, BANK), slice(BANK, S))
Y_COPY_ON_VECTOR = ()
Y_ROUND_ON_GPSIMD = (0,)
Y_ROUND_ON_SCALAR = (640, 896)
STORED_BY_BANK = ()
WORD_STORES = {1024: 0}


def tile_list_arrhenius_source_terms_kernel(
    tc, tab_words, tab_scales, offs, w1, gT, pre, wnu_words, wnu_scales, out_0, out_1, out_2
):
    nc = tc.nc

    with ExitStack() as ctx:
        keep = ctx.enter_context(tc.tile_pool(name="keep", bufs=1))
        hand = ctx.enter_context(tc.tile_pool(name="hand", bufs=1))
        psum = ctx.enter_context(tc.psum_pool(name="psum", bufs=1))

        def placed(shape, dtype, name, at):
            return hand.tile(shape, dtype, name=name, offset=at, align_bytes=64)

        def slot(i):
            return i * W + (0, 1024, 1024)[i] if i < 3 else i * W + 3072

        def bank(shape, number):
            return psum.tile(shape, F32, name="acc", tag="bank%d" % number)

        offsets = keep.tile([P, S // 16], U16, name="offsets")

        def listed(cols):
            return offsets[:, cols.start // 16 : cols.stop // 16]

        tab_plane = keep.tile([P, T], U8, name="tab_plane", align_bytes=64)
        wnu_plane_raw = placed([P, 2, N], U8, "wnu_plane_raw", W)
        wnu_raw = placed([P, 2, 2 * N], U8, "wnu_raw", slot(3) - 2048)
        nc.vector.memset(tab_plane[:].bitcast(I32), 0)
        nc.vector.memset(wnu_plane_raw[:].bitcast(I32), 0)

        g_rows = gT.rearrange("(b p t) c -> b t p c", p=P, t=PACK)
        windows, w_raw = {}, {}
        tab = [placed([P, T], I32, "tab%d" % a, slot(8 + a)) for a in range(2)]
        pre_rows = keep.tile([P, PASS], F32, name="pre_rows")
        identity = keep.tile([P, P], F32, name="identity")
        make_identity(nc, identity[:])
        nc.gpsimd.memset(pre_rows[:], 0.0)

        def load_g(b, t):
            windows[b, t] = placed([P, T], F32, "g_window%d%d" % (b, t), slot(b * PACK + t))
            nc.sync.dma_start(windows[b, t][:], g_rows[b, t])

        def load_w(a, b):
            w_raw[a, b] = placed([P, PACK, PASS], F32, "w_raw%d%d" % (a, b), slot(10 + 2 * b + a))
            rows = w1[a * PASS : (a + 1) * PASS, b * PASS : (b + 1) * PASS]
            nc.sync.dma_start(w_raw[a, b][:], rows.rearrange("(p j) c -> p j c", j=PACK))

        def load_tab(a):
            nc.sync.dma_start(tab[a][:], tab_words[a].rearrange("p c i -> p (c i)").bitcast(I32))

        def load_tab_scales(a):
            for r in range(PACK):
                nc.sync.dma_start(
                    tab_plane[PACK * a + r : P : 32, :].bitcast(I32),
                    tab_scales[a, r : 16 : PACK, :].bitcast(I32),
                )

        load_g(0, 0)
        nc.sync.dma_start(offsets[:], offs)
        load_tab_scales(0)
        load_tab(0)
        load_tab_scales(1)
        load_w(0, 0)
        load_w(1, 0)
        load_tab(1)
        nc.sync.dma_start(pre_rows[0:2, :], pre.rearrange("(b c) -> b c", b=2))
        for b, t in [(b, t) for b in range(2) for t in range(PACK)][1:]:
            load_g(b, t)
        load_w(0, 1)
        load_w(1, 1)
        nc.sync.dma_start(wnu_raw[:].bitcast(I32), wnu_words.rearrange("a p c -> p a c").bitcast(I32))
        for q in range(QUADS):
            nc.sync.dma_start(
                wnu_plane_raw[32 * q : 32 * q + 4].bitcast(I32),
                wnu_scales[:, 4 * q : 4 * q + 4, :].rearrange("a r c -> r a c").bitcast(I32),
            )

        inverse = [keep.tile([P, PACK, S], F32, name="inverse%d" % b) for b in range(2)]
        energy = [keep.tile([P, PACK, S], F32, name="energy%d" % b) for b in range(2)]
        gathered = {(b, t): inverse[b][:, t, :] for b in range(2) for t in range(PACK)}
        roots = dict(gathered)

        def gather_g(b, t, cols=slice(0, S)):
            nc.vector.tensor_copy(gathered[b, t][:, cols], windows[b, t][:].indirect(listed(cols)))

        def root_g(b, t, cols):
            nc.scalar.activation(roots[b, t][:, cols], gathered[b, t][:, cols], ACT.Abs_reciprocal_sqrt)

        def square_g(b, t, cols):
            nc.scalar.activation(inverse[b][:, t, cols], roots[b, t][:, cols], ACT.Square)

        def invert_g(b, t):
            for step in (root_g, square_g):
                for cols in HALVES:
                    step(b, t, cols)

        w_round, w_codes, w_scales = {}, {}, {}

        def round_w(a, b, *copies):
            grouped = placed([P, PASS * PACK], BF16, "w_round%d%d" % (a, b), slot(14) + a * W // 2)
            for pair, copy in zip(([slice(0, PACK)], [slice(0, 2), slice(2, 4)])[len(copies) - 1], copies):
                copy(
                    grouped[:].rearrange("p (t m j) -> p m j t", t=PACK, j=PACK)[:, :, :, pair],
                    w_raw[a, b][:].rearrange("p j (m t) -> p m j t", t=PACK)[:, :, :, pair],
                )
            w_round[a, b] = grouped

        def quantize_w(a, b):
            if (a, b) == (0, 0):
                codes = placed([P, PASS], I32, "w_codes00", slot(8))
            else:
                codes = keep.tile([P, PASS], I32, name="w_codes%d%d" % (a, b), align_bytes=64)
            scales = keep.tile([P, PASS], U8, name="w_scales%d%d" % (a, b), align_bytes=64)
            part = PASS if (a, b) == (1, 0) else PASS // 2
            for c0 in range(0, PASS, part):
                cols = slice(c0, c0 + part)
                nc.vector.quantize_mx(
                    codes[:, cols].bitcast(FP8X4), scales[:, cols], w_round[a, b][:, c0 * PACK : (c0 + part) * PACK]
                )
            w_codes[a, b], w_scales[a, b] = codes, scales

        picked = [keep.tile([P, S], I32, name="picked%d" % a, align_bytes=64) for a in range(2)]
        picked_plane = keep.tile([P, S], U8, name="picked_plane", align_bytes=64)

        def gather_tab(a, cols):
            nc.vector.tensor_copy(picked[a][:, cols].bitcast(U32), tab[a][:].bitcast(U32).indirect(listed(cols)))

        sums = {}

        def first_pass(a, b, t, cols, out, opens, closes):
            m_cols = slice(t * P, (t + 1) * P)
            nc.tensor.matmul_mx(
                out,
                lhsT=w_codes[a, b][:, m_cols].bitcast(FP8X4),
                lhsT_scale=w_scales[a, b][:, m_cols],
                rhs=picked[a][:, cols].bitcast(FP8X4),
                rhs_scale=picked_plane[4 * a : P, cols],
                start=opens,
                stop=closes,
            )

        def row_pass(a, b, t, h):
            if a == 0:
                sums[b, t, h] = bank([P, BANK], 2 * t + h)
            first_pass(a, b, t, HALVES[h], sums[b, t, h][:], a == 0, a == 1)

        def quarter_pass(a, k):
            cols = slice(256 * k, 256 * (k + 1))
            for t in range(PACK):
                if a == 0 and t % 2 == 0:
                    sums[k, t // 2] = bank([P, 2, 256], (2 * k + t // 2) % 6)
                first_pass(a, 1, t, cols, sums[k, t // 2][:, t % 2, :], (a, t % 2) == (0, 0), (a, t % 2) == (1, 1))

        def magnitude(b, t, h):
            nc.scalar.activation(energy[b][:, t, HALVES[h]], sums[b, t, h][:], ACT.Abs)

        def divide(out, b, t, cols=slice(0, S)):
            nc.gpsimd.tensor_tensor(out[:, cols], energy[b][:, t, cols], inverse[b][:, t, cols], ALU.mult)

        gather_g(0, 0)
        invert_g(0, 0)
        gather_tab(0, slice(0, S))
        nc.vector.tensor_copy(picked_plane[:], tab_plane[:].indirect(offsets[:]))
        round_w(0, 0, nc.scalar.copy, nc.scalar.copy)
        quantize_w(0, 0)
        round_w(1, 0, nc.scalar.copy, nc.vector.tensor_copy)
        quantize_w(1, 0)
        for h in range(2):
            gather_tab(1, HALVES[h])
        for t0 in (0, 2):
            for h in range(2):
                for a in range(2):
                    for t in (t0, t0 + 1):
                        row_pass(a, 0, t, h)
        for h in range(2):
            magnitude(0, 0, h)
            magnitude(0, 1, h)
            divide(energy[0][:, 0, :], 0, 0, HALVES[h])
        first, second = HALVES

        def square_on_gpsimd(out, roots_of):
            nc.gpsimd.tensor_tensor(out, roots_of, roots_of, ALU.mult)

        magnitude(0, 2, 0)
        gather_g(0, 1)
        for cols in HALVES:
            root_g(0, 1, cols)
            square_on_gpsimd(inverse[0][:, 1, cols], roots[0, 1][:, cols])
        divide(energy[0][:, 1, :], 0, 1)
        magnitude(0, 2, 1)
        magnitude(0, 3, 0)
        magnitude(0, 3, 1)
        factors = bank([P, PACK, P], 7)
        for t in range(PACK):
            nc.tensor.transpose(factors[:, t, :], pre_rows[:, t : PASS : PACK], identity[:])
        gather_g(0, 2)
        invert_g(0, 2)
        divide(energy[0][:, 2, :], 0, 2)
        gather_g(0, 3)
        for cols in HALVES:
            root_g(0, 3, cols)
        square_on_gpsimd(inverse[0][:, 3, :], roots[0, 3])
        divide(energy[0][:, 3, :], 0, 3)

        for t in range(2):
            gather_g(1, t)
            invert_g(1, t)
        spare_roots = keep.tile([P, 2, BANK], F32, name="spare_roots")
        gathered[1, 3] = placed([P, S], F32, "gathered13", slot(8))[:]
        gather_g(1, 2)
        for cols in HALVES:
            gather_g(1, 3, cols)
        root_g(1, 2, first)
        nc.scalar.activation(spare_roots[:, 0, :], gathered[1, 2][:, second], ACT.Abs_reciprocal_sqrt)
        roots[1, 3] = spare_roots[:, 1, :]
        root_g(1, 3, first)
        square_on_gpsimd(inverse[1][:, 2, first], roots[1, 2][:, first])
        square_g(1, 3, first)
        nc.scalar.activation(spare_roots[:, 1, :], gathered[1, 3][:, second], ACT.Abs_reciprocal_sqrt)
        for a in range(2):
            round_w(a, 1, nc.vector.tensor_copy, nc.vector.tensor_copy)
            quantize_w(a, 1)

        wnu_codes = placed([P, 2, PACK, 2 * P], U8, "wnu_codes", slot(14))
        wnu_plane = placed([P, 2, PACK, P], U8, "wnu_plane", slot(14) + 2048)
        nc.vector.tensor_copy(
            wnu_codes[:].bitcast(U16).rearrange("p a t m -> p a m t"),
            wnu_raw[:].bitcast(U16).rearrange("p a (m t) -> p a m t", t=PACK),
        )
        nc.vector.tensor_copy(
            wnu_plane[:].rearrange("p a t m -> p a m t"),
            wnu_plane_raw[:].rearrange("p a (m t) -> p a m t", t=PACK),
        )
        late_inverse = placed([P, 2, BANK], F32, "late_inverse", W // 2 + 64)
        square_on_gpsimd(late_inverse[:], spare_roots[:])
        for k in range(3):
            quarter_pass(0, k)
        for k in range(3):
            quarter_pass(1, k)

        def signed_ratio(k):
            cols = slice(256 * k, 256 * (k + 1))
            for i in range(2):
                pair = slice(2 * i, 2 * i + 2)
                nc.vector.tensor_tensor(energy[1][:, pair, cols], sums[k, i][:], inverse[1][:, pair, cols], ALU.mult)

        def late_magnitude(k, i):
            nc.scalar.activation(energy[1][:, 2 * i : 2 * i + 2, 256 * k : 256 * (k + 1)], sums[k, i][:], ACT.Abs)

        def late_ratio(out, k, i):
            cols = slice(256 * k, 256 * (k + 1))
            by = late_inverse[:, :, 256 * k - BANK : 256 * k - 256] if i else inverse[1][:, 0:2, cols]
            nc.gpsimd.tensor_tensor(out, energy[1][:, 2 * i : 2 * i + 2, cols], by, ALU.mult)

        decayed, h_round, h_codes, h_scales, y_sums, y_full, y_round = {}, {}, {}, {}, {}, {}, {}
        decayed0_at = {0: slot(8), 256: slot(12), 512: slot(12) + W // 2, 768: slot(8)}
        h_round_at = {0: slot(1) - 64, 256: slot(3) - 6080, 512: slot(3) - 64, 768: 0, 896: 2048}
        y_round_at = {0: h_round_at[512], 256: slot(12) - 4032, 512: slot(12) - 1984, 768: slot(9), 896: slot(9) + 1024}

        def share(b, cols, out):
            for unit in UNITS:
                if cols.start <= unit.start < cols.stop:
                    decayed[b, unit.start] = out[:, :, unit.start - cols.start : unit.stop - cols.start]

        def decay0(cols):
            out = placed([P, PACK, cols.stop - cols.start], F32, "decayed0_%d" % cols.start, decayed0_at[cols.start])
            nc.scalar.activation(out[:], energy[0][:, :, cols], ACT.Exp, scale=-1.0)
            share(0, cols, out)

        def unsign(cols):
            nc.scalar.activation(energy[1][:, :, cols], energy[1][:, :, cols], ACT.Abs)

        def decay1(cols):
            out = placed([P, PACK, cols.stop - cols.start], F32, "decayed1_%d" % cols.start, slot(10) + cols.start * 16)
            if cols.stop < S:
                nc.scalar.activation(out[:], energy[1][:, :, cols], ACT.Exp, scale=-1.0)
            else:
                nc.scalar.activation(out[:, 0:2, :], energy[1][:, 0:2, cols], ACT.Exp, scale=-1.0)
                nc.scalar.activation(out[:, 2:4, :], last_ratio[:], ACT.Exp, scale=-1.0)
            share(1, cols, out)

        def round_h(b, cols):
            width = cols.stop - cols.start
            if b == 0:
                h_round[cols.start] = placed([P, 2, width * PACK], BF16, "h_round%d" % cols.start, h_round_at[cols.start])
            nc.vector.tensor_tensor(
                h_round[cols.start][:, b, :].rearrange("p (c i t) -> p c t i", i=4, t=PACK),
                decayed[b, cols.start].rearrange("p t (c i) -> p c t i", i=4),
                factors[:, :, b].unsqueeze(1).unsqueeze(3).to_broadcast([P, width // 4, PACK, 4]),
                ALU.mult,
            )

        def quantize_h(cols):
            width = cols.stop - cols.start
            codes = keep.tile([P, 2 * width], I32, name="h_codes%d" % cols.start, align_bytes=64)
            scales = keep.tile([P, 2 * width], U8, name="h_scales%d" % cols.start, align_bytes=64)
            nc.vector.quantize_mx(codes[:].bitcast(FP8X4), scales[:], h_round[cols.start][:].rearrange("p b c -> p (b c)"))
            h_codes[cols.start], h_scales[cols.start] = codes, scales

        def second_product(cols):
            for c0 in range(cols.start, cols.stop, SUB):
                y_sums[c0] = bank([P, PACK, SUB], (6 + c0 // SUB) % 7)
                for b in range(2):
                    first_col = b * (cols.stop - cols.start) + c0 - cols.start
                    sub = slice(first_col, first_col + SUB)
                    for t in range(PACK):
                        nc.tensor.matmul_mx(
                            y_sums[c0][:, t, :],
                            lhsT=wnu_codes[:, b, t, :].bitcast(FP4X4),
                            lhsT_scale=wnu_plane[:, b, t, :],
                            rhs=h_codes[cols.start][:, sub].bitcast(FP8X4),
                            rhs_scale=h_scales[cols.start][:, sub],
                            start=(b == 0 and t == 0),
                            stop=(b == 1 and t == PACK - 1),
                        )

        y_rows = out_0.rearrange("(p t) c -> p t c", t=PACK)
        y_words = out_1[0].rearrange("p c t -> p (c t)").bitcast(I32)
        y_plane = placed([P, S], U8, "y_plane", h_round_at[896])
        y_codes = keep.tile([P, S], I32, name="y_codes", align_bytes=64)

        def copy_y(cols):
            width = cols.stop - cols.start
            y = placed([P, PACK, width], F32, "y%d" % cols.start, slot(4) + cols.start * 16)[:]
            for c0 in range(0, width, SUB):
                copy = nc.vector.tensor_copy if cols.start + c0 in Y_COPY_ON_VECTOR else nc.scalar.copy
                copy(y[:, :, c0 : c0 + SUB], y_sums[cols.start + c0][:])
                if cols.start in STORED_BY_BANK:
                    nc.sync.dma_start(y_rows[:, :, cols.start + c0 : cols.start + c0 + SUB], y[:, :, c0 : c0 + SUB])
            if cols.start not in STORED_BY_BANK:
                nc.sync.dma_start(y_rows[:, :, cols], y)
            for unit in UNITS:
                if cols.start <= unit.start < cols.stop:
                    y_full[unit.start] = y[:, :, unit.start - cols.start : unit.stop - cols.start]

        def round_y(cols):
            width = cols.stop - cols.start
            grouped = placed([P, width * PACK], BF16, "y_round%d" % cols.start, y_round_at[cols.start])
            if cols.start in Y_ROUND_ON_GPSIMD:
                for c0 in range(0, SUB, SUB):
                    nc.gpsimd.tensor_scalar(
                        grouped[:, c0 * PACK : (c0 + SUB) * PACK].rearrange("p (c i t) -> p c t i", i=4, t=PACK),
                        y_full[cols.start][:, :, c0 : c0 + SUB].rearrange("p t (c i) -> p c t i", i=4),
                        1.0,
                        0.0,
                        ALU.mult,
                        ALU.add,
                    )
            else:
                own = width - SUB * (cols.stop - SUB in Y_ROUND_ON_SCALAR)
                if own:
                    nc.vector.tensor_copy(
                        grouped[:, : own * PACK].rearrange("p (c i t) -> p c t i", i=4, t=PACK),
                        y_full[cols.start][:, :, :own].rearrange("p t (c i) -> p c t i", i=4),
                    )
                if own < width:
                    nc.scalar.copy(
                        grouped[:, own * PACK :].rearrange("p (c t) -> p c t", t=PACK),
                        y_sums[cols.stop - SUB][:].rearrange("p t c -> p c t"),
                    )
            y_round[cols.start] = grouped

        def quantize_y(cols):
            nc.vector.quantize_mx(y_codes[:, cols].bitcast(FP8X4), y_plane[:, cols], y_round[cols.start][:])
            if cols.stop in WORD_STORES:
                done = slice(WORD_STORES[cols.stop], cols.stop)
                nc.sync.dma_start(y_words[:, done], y_codes[:, done])

        def source_terms(cols):
            quantize_h(cols)
            second_product(cols)

        u0, u1, u2, u3, u4 = UNITS
        for cols in (u0, u1, u2):
            decay0(cols)
        signed_ratio(0)
        for a in range(2):
            quarter_pass(a, 3)
        signed_ratio(1)
        round_h(0, u0)
        round_h(0, u1)
        for i in range(2):
            late_magnitude(2, i)
            late_ratio(energy[1][:, 2 * i : 2 * i + 2, u2], 2, i)
        unsign(u0)
        decay1(u0)
        unsign(u1)
        round_h(0, u2)
        round_h(1, u0)
        source_terms(u0)
        last = slice(u3.start, u4.stop)
        last_ratio = placed([P, 2, 256], F32, "last_ratio", h_round_at[u0.start])
        decay1(u1)
        for i, out in enumerate((energy[1][:, 0:2, last], last_ratio[:])):
            late_magnitude(3, i)
            late_ratio(out, 3, i)
        round_h(1, u1)
        source_terms(u1)
        decay1(u2)
        decay0(last)
        round_h(1, u2)
        source_terms(u2)
        round_h(0, u3)
        copy_y(u0)
        round_y(u0)
        decay1(last)
        round_h(0, u4)
        round_h(1, u3)
        round_h(1, u4)
        source_terms(u3)
        source_terms(u4)
        copy_y(u1)
        copy_y(u2)
        nc.vector.tensor_copy(
            y_round[0][:, SUB * PACK :].rearrange("p (c i t) -> p c t i", i=4, t=PACK),
            y_full[0][:, :, SUB:].rearrange("p t (c i) -> p c t i", i=4),
        )
        round_y(u1)
        quantize_y(u0)
        round_y(u2)
        copy_y(last)
        quantize_y(u1)
        quantize_y(u2)
        round_y(u3)
        round_y(u4)
        quantize_y(u3)
        quantize_y(u4)
        for q in range(QUADS):
            nc.sync.dma_start(out_2[0, 4 * q : 4 * q + 4, :].bitcast(I32), y_plane[32 * q : 32 * q + 4, :].bitcast(I32))
